import numpy as np
import ml_dtypes


def mxq(x, axis, fmt="e4m3"):
    dtype, down = {"e4m3": (ml_dtypes.float8_e4m3fn, 7), "e5m2": (ml_dtypes.float8_e5m2, 14)}[fmt]
    v = np.moveaxis(np.asarray(x, np.float32).astype(ml_dtypes.bfloat16).astype(np.float64), axis, -1)
    blocks = v.reshape(v.shape[:-1] + (-1, 32))
    amax = np.abs(blocks).max(-1, keepdims=True)
    byte = np.maximum(np.where(amax > 0, np.frexp(amax)[1] - 1 + 127, 0) - down, 1)
    scale = np.exp2(byte - 127.0)
    codes = (blocks / scale).astype(np.float32).astype(dtype).astype(np.float64)
    return np.moveaxis((codes * scale).reshape(v.shape), -1, axis)


WIDE = False


def mx_kscale(k):
    if not WIDE:
        return np.ones(k)
    levels = np.array([10, -10, 5, -5, 0])
    if k % 512:
        return np.exp2(np.random.permutation(np.resize(levels, k // 32))).repeat(32)
    a = np.empty((k // 512, 16))
    for p in range(k // 512):
        a[p, :8] = np.random.permutation(np.resize(levels, 8))
        for g in range(8):
            far = levels[np.abs(levels - a[p, g]) >= 10]
            a[p, g + 8] = far[np.random.randint(len(far))]
    return np.exp2(a.ravel()).repeat(32)


def f64(x):
    return np.asarray(x).astype(np.float64)


def striped(idx):
    return np.tile(idx.reshape(-1, 16).T, (8, 1)).astype(np.uint16)


def unstriped(offs):
    return offs[:16].T.reshape(-1).astype(np.int64)


E2M1 = np.array([0.0, 0.5, 1.0, 1.5, 2.0, 3.0, 4.0, 6.0, -0.0, -0.5, -1.0, -1.5, -2.0, -3.0, -4.0, -6.0])


def pack_weight(w, fmt):
    k, n = w.shape
    w = f64(np.asarray(w, np.float32).astype(ml_dtypes.bfloat16)).reshape(k // 32, 32, n)
    amax = np.abs(w).max(1)
    if fmt == "e4m3":
        byte = np.frexp(amax)[1] - 1 + 127 - 7
    else:
        mant, ex = np.frexp(amax / 6.0)
        byte = np.where(mant > 0.5, ex, ex - 1) + 127
    byte = np.clip(np.where(amax > 0, byte, 1), 1, 254)
    scaled = (w * np.exp2(127.0 - byte)[:, None, :]).reshape(k, n).astype(np.float32)
    by_word = np.ascontiguousarray(scaled.reshape(k // 512, 128, 4, n).transpose(0, 1, 3, 2))
    if fmt == "e4m3":
        words = by_word.astype(ml_dtypes.float8_e4m3fn).view(np.uint8)
    else:
        c = by_word.astype(ml_dtypes.float4_e2m1fn).view(np.uint8) & 0xF
        words = (c[..., 0::2] | (c[..., 1::2] << 4)).reshape(k // 512, 128, 2 * n)
    return np.ascontiguousarray(words), np.ascontiguousarray(byte.astype(np.uint8).reshape(k // 512, 16, n))


def unpack_weight(words, scales, fmt):
    g, _, n = scales.shape
    words = np.ascontiguousarray(words).reshape(g, 128, n, -1)
    if fmt == "e4m3":
        vals = words.view(ml_dtypes.float8_e4m3fn).astype(np.float64)
    else:
        nib = np.empty((g, 128, n, 4), np.uint8)
        nib[..., 0::2] = words & 0xF
        nib[..., 1::2] = words >> 4
        vals = E2M1[nib]
    vals = vals * np.repeat(np.exp2(scales.astype(np.float64) - 127.0), 8, axis=1)[..., None]
    return vals.transpose(0, 1, 3, 2).reshape(g * 512, n)


def gelu(v):
    return 0.5 * v * (1.0 + np.tanh(np.sqrt(2.0 / np.pi) * (v + 0.044715 * v**3)))


K, K3, H, N, T, T2, T3, S = 1024, 512, 1024, 384, 2048, 1024, 2048, 512

def setup_inputs():
    n = np.random.standard_normal
    s = mx_kscale(K)[:, None]
    s3 = mx_kscale(K3)[:, None]
    u = mx_kscale(H)[:, None]
    tab_words, tab_scales = pack_weight(n((K, T)) * s, "e4m3")
    tab2_words, tab2_scales = pack_weight(n((K, T2)) * s, "e4m3")
    tab3_words, tab3_scales = pack_weight(n((K3, T3)) * s3, "e2m1")
    w1_words, w1_scales = pack_weight(n((K, H)) * np.sqrt(0.5 / K) / s, "e2m1")
    w3_words, w3_scales = pack_weight(0.3 * n((K3, H)) / np.sqrt(K3) / s3, "e4m3")
    return {
        "tab_words": tab_words, "tab_scales": tab_scales,
        "tab2_words": tab2_words, "tab2_scales": tab2_scales,
        "tab3_words": tab3_words, "tab3_scales": tab3_scales,
        "offs": striped(np.random.permutation(T)[:S]),
        "offs2": striped(np.random.permutation(T2)[:S]),
        "offs3": striped(np.random.permutation(T3)[:S]),
        "w1_words": w1_words, "w1_scales": w1_scales,
        "w2": (n((K, H)) * np.sqrt(0.5 / K) / s).astype(np.float32),
        "w3_words": w3_words, "w3_scales": w3_scales,
        "gain": (np.exp(0.3 * n(H)) * u[:, 0]).astype(np.float32),
        "w4": (n((H, N)) / np.sqrt(H) / u).astype(np.float32),
        "bias": (0.5 * n(N)).astype(np.float32),
    }

def reference(tab_words, tab_scales, tab2_words, tab2_scales, tab3_words, tab3_scales, offs, offs2, offs3,
              w1_words, w1_scales, w2, w3_words, w3_scales, gain, w4, bias):
    v = unpack_weight(tab_words, tab_scales, "e4m3")[:, unstriped(offs)]
    v2 = unpack_weight(tab2_words, tab2_scales, "e4m3")[:, unstriped(offs2)]
    v3 = unpack_weight(tab3_words, tab3_scales, "e2m1")[:, unstriped(offs3)]
    lig = unpack_weight(w1_words, w1_scales, "e2m1").T @ v
    poc = mxq(f64(w2), 0, "e4m3").T @ v2
    sol = unpack_weight(w3_words, w3_scales, "e4m3").T @ v3
    h = np.square(lig - poc) * np.exp(sol) * f64(gain)[:, None]
    y = mxq(f64(w4), 0, "e4m3").T @ mxq(h, 0, "e4m3")
    return y + f64(bias)[:, None]

@@ -1,0 +1,303 @@
+from contextlib import ExitStack
+
+import concourse.mybir as mybir
+from concourse.masks import make_identity
+
+K, K3, H, N, T, T2, T3, S = 1024, 512, 1024, 384, 2048, 1024, 2048, 512
+FLOPS = 2 * S * (2 * K * H + K3 * H + H * N)
+
+F32 = mybir.dt.float32
+BF16 = mybir.dt.bfloat16
+I32 = mybir.dt.int32
+U32 = mybir.dt.uint32
+U16 = mybir.dt.uint16
+U8 = mybir.dt.uint8
+FP8X4 = mybir.dt.float8_e4m3fn_x4
+FP4X4 = mybir.dt.float4_e2m1fn_x4
+ACT = mybir.ActivationFunctionType
+ALU = mybir.AluOpType
+
+P = 128
+PACK = 4
+KP = P * PACK
+HALF = S // 2
+
+
+def tile_list_solvent_docking_rescoring_kernel(
+    tc, tab_words, tab_scales, tab2_words, tab2_scales, tab3_words, tab3_scales, offs, offs2, offs3,
+    w1_words, w1_scales, w2, w3_words, w3_scales, gain, w4, bias, out,
+):
+    nc = tc.nc
+    with ExitStack() as ctx:
+        sb = ctx.enter_context(tc.tile_pool(name="sb", bufs=1))
+        psum = ctx.enter_context(tc.psum_pool(name="psum", bufs=1))
+
+        def alloc(name, shape, dtype):
+            return sb.tile(shape, dtype, name=name, align_bytes=64)
+
+        def bank(index, name):
+            return psum.tile([P, S], F32, name=name, tag="bank%d" % index)
+
+        def zeroed_plane(engine, name, width):
+            plane = alloc(name, [P, width], U8)
+            engine.memset(plane[:].bitcast(I32), 0)
+            return plane
+
+        def load_list(name, src):
+            offsets = sb.tile([P, S // 16], U16, name=name)
+            nc.sync.dma_start(offsets[:], src)
+            return offsets
+
+        def load_scale_rows(queue, plane, scales):
+            passes = scales.shape[0]
+            rows = scales.bitcast(I32).rearrange("a (q r) w -> r q a w", r=4)
+            for r in range(4):
+                queue.dma_start(plane[r:P:32, :].bitcast(I32).rearrange("q (a w) -> q a w", a=passes), rows[r])
+
+        def load_words(name, src, width, dtype):
+            words = alloc(name, [P, width], dtype)
+            nc.sync.dma_start(words[:].bitcast(I32), src.bitcast(I32))
+            return words
+
+        def gather(name, window, offsets, dtype):
+            picked = alloc(name, [P, S], dtype)
+            nc.vector.tensor_copy(picked[:], window.indirect(offsets[:]))
+            return picked
+
+        def reorder(name, src, width, dtype, run):
+            ordered = alloc(name, [P, width], dtype)
+            nc.vector.tensor_copy(
+                ordered[:].bitcast(I32).rearrange("p (g t m w) -> p g t m w", t=4, m=32, w=run),
+                src[:].bitcast(I32).rearrange("p (g m t w) -> p g t m w", t=4, m=32, w=run),
+            )
+            return ordered
+
+        def reorder_plane(name, src, width):
+            ordered = alloc(name, [P, width], U8)
+            nc.vector.tensor_copy(
+                ordered[:].bitcast(I32).rearrange("p (g t m) -> p g t m", t=4, m=32),
+                src[:].bitcast(I32).rearrange("p (g m t) -> p g t m", t=4, m=32),
+            )
+            return ordered
+
+        tab3_plane = zeroed_plane(nc.vector, "tab3_plane", T3)
+        w3_plane = zeroed_plane(nc.vector, "w3_plane", H)
+        tab2_plane = zeroed_plane(nc.vector, "tab2_plane", T2)
+        tab_plane = zeroed_plane(nc.vector, "tab_plane", 2 * T)
+        w1_plane = zeroed_plane(nc.vector, "w1_plane", 2 * H)
+
+        rows = alloc("rows", [P, P], F32)
+        nc.gpsimd.memset(rows[:], 0.0)
+        gain_rows = gain.rearrange("(b m t l) -> b t m l", b=2, t=4, l=4)
+        for b in range(2):
+            nc.gpsimd.dma_start(rows[4 * b : 4 * b + 4, :].rearrange("t (m l) -> t m l", l=4), gain_rows[b])
+        nc.gpsimd.dma_start(rows[8:11, :], bias.rearrange("(c p) -> c p", p=P))
+        ident = alloc("ident", [P, P], F32)
+        make_identity(nc, ident[:])
+        halves = alloc("halves", [P, 8], F32)
+        nc.gpsimd.memset(halves[:], 0.5)
+
+        tab2_w = [None, None]
+        tab_w = [None, None]
+        w2_raw = {}
+        w4_raw = [None, None]
+
+        def load_w2(b, a):
+            raw = alloc("w2_raw%d%d" % (b, a), [P, PACK, KP], F32)
+            nc.sync.dma_start(raw[:], w2[a * KP : (a + 1) * KP, b * KP : (b + 1) * KP].rearrange("(p j) c -> p j c", j=PACK))
+            w2_raw[(b, a)] = raw
+
+        def load_w4(b):
+            raw = alloc("w4_raw%d" % b, [P, PACK, N], F32)
+            src = w4[b * KP : (b + 1) * KP, :].rearrange("(m t l) n -> t m l n", t=4, l=4)
+            for t in range(4):
+                nc.sync.dma_start(raw[:, t, :], src[t])
+            w4_raw[b] = raw
+
+        idx3 = load_list("idx3", offs3)
+        tab3_w = load_words("tab3_w", tab3_words[0], T3, U16)
+        w3_w = load_words("w3_w", w3_words[0].rearrange("p c i -> p (c i)"), H, U32)
+        load_scale_rows(nc.sync, tab3_plane, tab3_scales)
+        load_scale_rows(nc.sync, w3_plane, w3_scales)
+        idx2 = load_list("idx2", offs2)
+        tab2_w[0] = load_words("tab2_w0", tab2_words[0].rearrange("p c i -> p (c i)"), T2, U32)
+        tab2_rows = tab2_scales.bitcast(I32)
+        for q in range(4):
+            nc.sync.dma_start(tab2_plane[32 * q + 4 : 32 * q + 12, :].bitcast(I32), tab2_rows[:, 4 * q : 4 * q + 4, :])
+        load_w2(0, 0)
+        tab2_w[1] = load_words("tab2_w1", tab2_words[1].rearrange("p c i -> p (c i)"), T2, U32)
+        idx = load_list("idx", offs)
+        tab_w[0] = load_words("tab_w0", tab_words[0].rearrange("p c i -> p (c i)"), T, U32)
+        load_scale_rows(nc.sync, tab_plane, tab_scales)
+        w1_w = alloc("w1_w", [P, 2 * 2 * H], U8)
+        nc.sync.dma_start(
+            w1_w[:].bitcast(I32).rearrange("p (a w) -> p a w", a=2), w1_words.bitcast(I32).rearrange("a p w -> p a w")
+        )
+        load_scale_rows(nc.sync, w1_plane, w1_scales)
+        tab_w[1] = load_words("tab_w1", tab_words[1].rearrange("p c i -> p (c i)"), T, U32)
+        load_w2(0, 1)
+        load_w2(1, 0)
+        load_w2(1, 1)
+        load_w4(0)
+        load_w4(1)
+
+        turned = bank(7, "turned")
+        nc.tensor.transpose(turned[:, 0:P], rows[:], ident[:])
+        cols = alloc("cols", [P, 16], F32)
+        nc.vector.tensor_copy(cols[:], turned[:, 0:16])
+        root_gain = alloc("root_gain", [P, 8], F32)
+        nc.gpsimd.tensor_tensor(root_gain[:], cols[:, 0:8], halves[:], ALU.pow)
+
+        v3_w = gather("v3_w", tab3_w[:], idx3, U16)
+        w3_o = reorder("w3_o", w3_w, H, U32, 4)
+        v3_s = gather("v3_s", tab3_plane[:], idx3, U8)
+        w3_s = reorder_plane("w3_s", w3_plane, H)
+        damp = alloc("damp", [P, 8, S], F32)
+        for g in range(8):
+            cs = slice(g * P, (g + 1) * P)
+            sol = bank(4 + g % 4, "sol%d" % g)
+            nc.tensor.matmul_mx(
+                sol[:], lhsT=w3_o[:, cs].bitcast(FP8X4), lhsT_scale=w3_s[:, cs],
+                rhs=v3_w[:].bitcast(FP4X4), rhs_scale=v3_s[:], start=True, stop=True,
+            )
+            nc.scalar.activation(damp[:, g, :], sol[:], ACT.Exp, scale=0.5)
+
+        w2_c = {}
+        w2_s = {}
+
+        def quantise_w2(b, a, on_vector):
+            grouped = alloc("w2_g%d%d" % (b, a), [P, PACK * KP], BF16)
+            src = w2_raw[(b, a)][:].rearrange("p j (m t l) -> p t m j l", t=4, l=4)
+            dst = grouped[:].rearrange("p (t m l j) -> p t m j l", t=4, l=4, j=PACK)
+            for t in range(4):
+                if t in on_vector:
+                    nc.vector.tensor_scalar(dst[:, t], src[:, t], -1.0, None, ALU.mult)
+                else:
+                    nc.scalar.activation(dst[:, t], src[:, t], ACT.Copy, scale=-1.0)
+            codes = alloc("w2_c%d%d" % (b, a), [P, KP], U32)
+            scales = alloc("w2_s%d%d" % (b, a), [P, KP], U8)
+            nc.vector.quantize_mx(codes[:].bitcast(FP8X4), scales[:], grouped[:])
+            w2_c[(b, a)] = codes
+            w2_s[(b, a)] = scales
+
+        v2_w = [None, None]
+        v2_w[0] = gather("v2_w0", tab2_w[0][:], idx2, U32)
+        v2_s = gather("v2_s", tab2_plane[:], idx2, U8)
+        v2_w[1] = gather("v2_w1", tab2_w[1][:], idx2, U32)
+        quantise_w2(0, 0, ())
+        v_w = [None, None]
+        v_s = [None, None]
+        v_w[0] = gather("v_w0", tab_w[0][:], idx, U32)
+        v_s[0] = gather("v_s0", tab_plane[:, 0:T], idx, U8)
+        w1_o = reorder("w1_o", w1_w, 2 * 2 * H, U8, 2)
+        w1_s = reorder_plane("w1_s", w1_plane, 2 * H)
+        v_s[1] = gather("v_s1", tab_plane[:, T : 2 * T], idx, U8)
+        v_w[1] = gather("v_w1", tab_w[1][:], idx, U32)
+        quantise_w2(0, 1, ())
+
+        def ligand_pass(acc, g, a, start, stop):
+            c0 = a * H + g * P
+            nc.tensor.matmul_mx(
+                acc[:], lhsT=w1_o[:, 2 * c0 : 2 * (c0 + P)].bitcast(FP4X4), lhsT_scale=w1_s[:, c0 : c0 + P],
+                rhs=v_w[a][:].bitcast(FP8X4), rhs_scale=v_s[a][:], start=start, stop=stop,
+            )
+
+        def pocket_pass(acc, b, t, a, start, stop):
+            cs = slice(t * P, (t + 1) * P)
+            nc.tensor.matmul_mx(
+                acc[:], lhsT=w2_c[(b, a)][:, cs].bitcast(FP8X4), lhsT_scale=w2_s[(b, a)][:, cs],
+                rhs=v2_w[a][:].bitcast(FP8X4), rhs_scale=v2_s[4 + 4 * a : P, :], start=start, stop=stop,
+            )
+
+        w4_c = [None, None]
+        w4_s = [None, None]
+
+        def quantise_w4(b):
+            grouped = alloc("w4_g%d" % b, [P, PACK * N], BF16)
+            nc.vector.tensor_copy(
+                grouped[:].rearrange("p (c l t) -> p c t l", l=4, t=PACK),
+                w4_raw[b][:].rearrange("p t (c l) -> p c t l", l=4),
+            )
+            codes = alloc("w4_c%d" % b, [P, N], U32)
+            scales = alloc("w4_s%d" % b, [P, N], U8)
+            for c0, c1 in ((0, 256), (256, N)):
+                nc.vector.quantize_mx(codes[:, c0:c1].bitcast(FP8X4), scales[:, c0:c1], grouped[:, PACK * c0 : PACK * c1])
+            w4_c[b] = codes
+            w4_s[b] = scales
+
+        h_c = {}
+        h_s = {}
+
+        def make_root(b, diff, pieces):
+            root = alloc("root%d" % b, [P, PACK, S], F32)
+            width = S // pieces
+            for piece in range(pieces):
+                js = slice(piece * width, (piece + 1) * width)
+                for t in range(4):
+                    g = 4 * b + t
+                    nc.vector.scalar_tensor_tensor(
+                        root[:, t, js], diff[t][:, js], root_gain[:, g : g + 1], damp[:, g, js], ALU.mult, ALU.mult
+                    )
+            return root
+
+        def make_h(b, root):
+            grouped = alloc("h_g%d" % b, [P, PACK * S], BF16)
+            codes = alloc("h_c%d" % b, [P, S], U32)
+            scales = alloc("h_s%d" % b, [P, S], U8)
+            for half in range(2):
+                js = slice(half * HALF, (half + 1) * HALF)
+                gs = slice(PACK * half * HALF, PACK * (half + 1) * HALF)
+                nc.scalar.activation(
+                    grouped[:, gs].rearrange("p (c l t) -> p c t l", l=4, t=PACK),
+                    root[:, :, js].rearrange("p t (c l) -> p c t l", l=4),
+                    ACT.Square,
+                )
+                nc.vector.quantize_mx(codes[:, js].bitcast(FP8X4), scales[:, js], grouped[:, gs])
+            h_c[b] = codes
+            h_s[b] = scales
+
+        diff0 = [bank(t, "diff0%d" % t) for t in range(4)]
+        diff1 = [bank(4 + t, "diff1%d" % t) for t in range(4)]
+        for t in range(4):
+            pocket_pass(diff0[t], 0, t, 0, True, False)
+        for a in range(2):
+            for t in range(4):
+                ligand_pass(diff0[t], t, a, False, False)
+            for t in range(4):
+                ligand_pass(diff1[t], 4 + t, a, a == 0, False)
+        for t in range(4):
+            pocket_pass(diff0[t], 0, t, 1, False, True)
+        root0 = make_root(0, diff0, 1)
+        for a in range(2):
+            quantise_w2(1, a, (0, 1) if a == 1 else ())
+            for t in range(4):
+                pocket_pass(diff1[t], 1, t, a, False, a == 1)
+        make_h(0, root0)
+        root1 = make_root(1, diff1, 2)
+        quantise_w4(0)
+        quantise_w4(1)
+        make_h(1, root1)
+
+        out_view = out.rearrange("(c p) j -> p c j", p=P)
+        accs = [[bank(2 * half + i, "y%d%d" % (half, i)) for i in range(2)] for half in range(2)]
+        for b in range(2):
+            for half in range(2):
+                js = slice(half * HALF, (half + 1) * HALF)
+                for c in range(3):
+                    ns = slice(c * P, (c + 1) * P)
+                    nc.tensor.matmul_mx(
+                        accs[half][c // 2][:, (c % 2) * HALF : (c % 2 + 1) * HALF],
+                        lhsT=w4_c[b][:, ns].bitcast(FP8X4), lhsT_scale=w4_s[b][:, ns],
+                        rhs=h_c[b][:, js].bitcast(FP8X4), rhs_scale=h_s[b][:, js],
+                        start=(b == 0 and c != 1), stop=(b == 1 and c != 0),
+                    )
+        for half in range(2):
+            js = slice(half * HALF, (half + 1) * HALF)
+            result = alloc("result%d" % half, [P, 3, HALF], F32)
+            for c in range(3):
+                src = accs[half][c // 2][:, (c % 2) * HALF : (c % 2 + 1) * HALF]
+                if c == 2:
+                    nc.vector.tensor_scalar(result[:, c, :], src, cols[:, 8 + c : 9 + c], None, ALU.add)
+                else:
+                    nc.scalar.activation(result[:, c, :], src, ACT.Identity, bias=cols[:, 8 + c : 9 + c])
+            nc.sync.dma_start(out_view[:, :, js], result[:])

@@ -32,8 +32,8 @@ def tile_list_solvent_docking_rescoring_kernel(
         sb = ctx.enter_context(tc.tile_pool(name="sb", bufs=1))
         psum = ctx.enter_context(tc.psum_pool(name="psum", bufs=1))
 
-        def alloc(name, shape, dtype):
-            return sb.tile(shape, dtype, name=name, align_bytes=64)
+        def alloc(name, shape, dtype, slot=None):
+            return sb.tile(shape, dtype, name=name, tag=slot or name, align_bytes=64)
 
         def bank(index, name):
             return psum.tile([P, S], F32, name=name, tag="bank%d" % index)
@@ -59,8 +59,8 @@ def tile_list_solvent_docking_rescoring_kernel(
             nc.sync.dma_start(words[:].bitcast(I32), src.bitcast(I32))
             return words
 
-        def gather(name, window, offsets, dtype):
-            picked = alloc(name, [P, S], dtype)
+        def gather(name, window, offsets, dtype, slot=None):
+            picked = alloc(name, [P, S], dtype, slot)
             nc.vector.tensor_copy(picked[:], window.indirect(offsets[:]))
             return picked
 
@@ -80,22 +80,16 @@ def tile_list_solvent_docking_rescoring_kernel(
             )
             return ordered
 
-        tab3_plane = zeroed_plane(nc.vector, "tab3_plane", T3)
-        w3_plane = zeroed_plane(nc.vector, "w3_plane", H)
-        tab2_plane = zeroed_plane(nc.vector, "tab2_plane", T2)
+        tab3_plane = zeroed_plane(nc.gpsimd, "tab3_plane", T3)
+        w3_plane = zeroed_plane(nc.gpsimd, "w3_plane", H)
         tab_plane = zeroed_plane(nc.vector, "tab_plane", 2 * T)
+        tab2_plane = zeroed_plane(nc.vector, "tab2_plane", T2)
         w1_plane = zeroed_plane(nc.vector, "w1_plane", 2 * H)
 
-        rows = alloc("rows", [P, P], F32)
+        rows = alloc("rows", [P, 2 * P], F32)
         nc.gpsimd.memset(rows[:], 0.0)
-        gain_rows = gain.rearrange("(b m t l) -> b t m l", b=2, t=4, l=4)
-        for b in range(2):
-            nc.gpsimd.dma_start(rows[4 * b : 4 * b + 4, :].rearrange("t (m l) -> t m l", l=4), gain_rows[b])
-        nc.gpsimd.dma_start(rows[8:11, :], bias.rearrange("(c p) -> c p", p=P))
         ident = alloc("ident", [P, P], F32)
         make_identity(nc, ident[:])
-        halves = alloc("halves", [P, 8], F32)
-        nc.gpsimd.memset(halves[:], 0.5)
 
         tab2_w = [None, None]
         tab_w = [None, None]
@@ -115,52 +109,58 @@ def tile_list_solvent_docking_rescoring_kernel(
             w4_raw[b] = raw
 
         idx3 = load_list("idx3", offs3)
+        idx = load_list("idx", offs)
         tab3_w = load_words("tab3_w", tab3_words[0], T3, U16)
         w3_w = load_words("w3_w", w3_words[0].rearrange("p c i -> p (c i)"), H, U32)
         load_scale_rows(nc.sync, tab3_plane, tab3_scales)
-        load_scale_rows(nc.sync, w3_plane, w3_scales)
-        idx2 = load_list("idx2", offs2)
-        tab2_w[0] = load_words("tab2_w0", tab2_words[0].rearrange("p c i -> p (c i)"), T2, U32)
-        tab2_rows = tab2_scales.bitcast(I32)
-        for q in range(4):
-            nc.sync.dma_start(tab2_plane[32 * q + 4 : 32 * q + 12, :].bitcast(I32), tab2_rows[:, 4 * q : 4 * q + 4, :])
-        load_w2(0, 0)
-        tab2_w[1] = load_words("tab2_w1", tab2_words[1].rearrange("p c i -> p (c i)"), T2, U32)
-        idx = load_list("idx", offs)
         tab_w[0] = load_words("tab_w0", tab_words[0].rearrange("p c i -> p (c i)"), T, U32)
+        load_scale_rows(nc.sync, w3_plane, w3_scales)
+        nc.sync.dma_start(rows[0:4, :].rearrange("t (m l) -> t m l", l=4), gain.rearrange("(m t l) -> t m l", t=4, l=4))
+        nc.sync.dma_start(rows[4:7, 0:P], bias.rearrange("(c p) -> c p", p=P))
+        load_w2(0, 0)
         load_scale_rows(nc.sync, tab_plane, tab_scales)
         w1_w = alloc("w1_w", [P, 2 * 2 * H], U8)
         nc.sync.dma_start(
             w1_w[:].bitcast(I32).rearrange("p (a w) -> p a w", a=2), w1_words.bitcast(I32).rearrange("a p w -> p a w")
         )
+        tab2_w[0] = load_words("tab2_w0", tab2_words[0].rearrange("p c i -> p (c i)"), T2, U32)
         load_scale_rows(nc.sync, w1_plane, w1_scales)
+        idx2 = load_list("idx2", offs2)
         tab_w[1] = load_words("tab_w1", tab_words[1].rearrange("p c i -> p (c i)"), T, U32)
+        tab2_rows = tab2_scales.bitcast(I32)
+        for q in range(4):
+            nc.sync.dma_start(tab2_plane[32 * q + 4 : 32 * q + 12, :].bitcast(I32), tab2_rows[:, 4 * q : 4 * q + 4, :])
         load_w2(0, 1)
+        tab2_w[1] = load_words("tab2_w1", tab2_words[1].rearrange("p c i -> p (c i)"), T2, U32)
         load_w2(1, 0)
         load_w2(1, 1)
         load_w4(0)
         load_w4(1)
 
+
         turned = bank(7, "turned")
-        nc.tensor.transpose(turned[:, 0:P], rows[:], ident[:])
-        cols = alloc("cols", [P, 16], F32)
-        nc.vector.tensor_copy(cols[:], turned[:, 0:16])
-        root_gain = alloc("root_gain", [P, 8], F32)
-        nc.gpsimd.tensor_tensor(root_gain[:], cols[:, 0:8], halves[:], ALU.pow)
+        for b in range(2):
+            nc.tensor.transpose(turned[:, b * P : (b + 1) * P], rows[:, b * P : (b + 1) * P], ident[:])
+        columns = turned[:, 0 : 2 * P].rearrange("p (b c) -> p b c", b=2)
+        root_gain = alloc("root_gain", [P, 2, 4], F32)
+        nc.scalar.activation(root_gain[:], columns[:, :, 0:4], ACT.Sqrt)
+        bias_cols = alloc("bias_cols", [P, 3], F32)
+        nc.scalar.copy(bias_cols[:], turned[:, 4:7])
 
         v3_w = gather("v3_w", tab3_w[:], idx3, U16)
         w3_o = reorder("w3_o", w3_w, H, U32, 4)
         v3_s = gather("v3_s", tab3_plane[:], idx3, U8)
         w3_s = reorder_plane("w3_s", w3_plane, H)
-        damp = alloc("damp", [P, 8, S], F32)
+        damp = [alloc("damp%d" % g, [P, S], F32) for g in range(8)]
         for g in range(8):
             cs = slice(g * P, (g + 1) * P)
-            sol = bank(4 + g % 4, "sol%d" % g)
+            sol = bank(g, "sol%d" % g)
             nc.tensor.matmul_mx(
                 sol[:], lhsT=w3_o[:, cs].bitcast(FP8X4), lhsT_scale=w3_s[:, cs],
                 rhs=v3_w[:].bitcast(FP4X4), rhs_scale=v3_s[:], start=True, stop=True,
             )
-            nc.scalar.activation(damp[:, g, :], sol[:], ACT.Exp, scale=0.5)
+            nc.scalar.activation(damp[g][:], sol[:], ACT.Exp, scale=0.5)
+
 
         w2_c = {}
         w2_s = {}
@@ -180,19 +180,17 @@ def tile_list_solvent_docking_rescoring_kernel(
             w2_c[(b, a)] = codes
             w2_s[(b, a)] = scales
 
+        v_w = [None, None]
+        v_w[0] = gather("v_w0", tab_w[0][:], idx, U32)
+        w1_o = reorder("w1_o", w1_w, 2 * 2 * H, U8, 2)
+        v_s = [gather("v_s%d" % a, tab_plane[:, a * T : (a + 1) * T], idx, U8) for a in range(2)]
+        w1_s = reorder_plane("w1_s", w1_plane, 2 * H)
         v2_w = [None, None]
         v2_w[0] = gather("v2_w0", tab2_w[0][:], idx2, U32)
-        v2_s = gather("v2_s", tab2_plane[:], idx2, U8)
-        v2_w[1] = gather("v2_w1", tab2_w[1][:], idx2, U32)
-        quantise_w2(0, 0, ())
-        v_w = [None, None]
-        v_s = [None, None]
-        v_w[0] = gather("v_w0", tab_w[0][:], idx, U32)
-        v_s[0] = gather("v_s0", tab_plane[:, 0:T], idx, U8)
-        w1_o = reorder("w1_o", w1_w, 2 * 2 * H, U8, 2)
-        w1_s = reorder_plane("w1_s", w1_plane, 2 * H)
-        v_s[1] = gather("v_s1", tab_plane[:, T : 2 * T], idx, U8)
         v_w[1] = gather("v_w1", tab_w[1][:], idx, U32)
+        v2_s = gather("v2_s", tab2_plane[:], idx2, U8)
+        quantise_w2(0, 0, ())
+        v2_w[1] = gather("v2_w1", tab2_w[1][:], idx2, U32)
         quantise_w2(0, 1, ())
 
         def ligand_pass(acc, g, a, start, stop):
@@ -212,13 +210,16 @@ def tile_list_solvent_docking_rescoring_kernel(
         w4_c = [None, None]
         w4_s = [None, None]
 
-        def quantise_w4(b):
-            grouped = alloc("w4_g%d" % b, [P, PACK * N], BF16)
-            nc.vector.tensor_copy(
+        def round_w4(b, copy, slot):
+            grouped = alloc("w4_g%d" % b, [P, PACK * N], BF16, slot)
+            copy(
                 grouped[:].rearrange("p (c l t) -> p c t l", l=4, t=PACK),
                 w4_raw[b][:].rearrange("p t (c l) -> p c t l", l=4),
             )
-            codes = alloc("w4_c%d" % b, [P, N], U32)
+            return grouped
+
+        def quantise_w4(b, grouped, slot):
+            codes = alloc("w4_c%d" % b, [P, N], U32, slot)
             scales = alloc("w4_s%d" % b, [P, N], U8)
             for c0, c1 in ((0, 256), (256, N)):
                 nc.vector.quantize_mx(codes[:, c0:c1].bitcast(FP8X4), scales[:, c0:c1], grouped[:, PACK * c0 : PACK * c1])
@@ -229,75 +230,84 @@ def tile_list_solvent_docking_rescoring_kernel(
         h_s = {}
 
         def make_root(b, diff, pieces):
-            root = alloc("root%d" % b, [P, PACK, S], F32)
+            roots = []
             width = S // pieces
             for piece in range(pieces):
                 js = slice(piece * width, (piece + 1) * width)
+                root = alloc("root%d%d" % (b, piece), [P, PACK, width], F32)
                 for t in range(4):
                     g = 4 * b + t
                     nc.vector.scalar_tensor_tensor(
-                        root[:, t, js], diff[t][:, js], root_gain[:, g : g + 1], damp[:, g, js], ALU.mult, ALU.mult
+                        root[:, t, :], diff[t][:, js], root_gain[:, b, t : t + 1], damp[g][:, js], ALU.mult, ALU.mult
                     )
-            return root
+                for j0 in range(0, width, HALF):
+                    roots.append(root[:, :, j0 : j0 + HALF])
+            return roots
 
-        def make_h(b, root):
-            grouped = alloc("h_g%d" % b, [P, PACK * S], BF16)
-            codes = alloc("h_c%d" % b, [P, S], U32)
-            scales = alloc("h_s%d" % b, [P, S], U8)
-            for half in range(2):
-                js = slice(half * HALF, (half + 1) * HALF)
-                gs = slice(PACK * half * HALF, PACK * (half + 1) * HALF)
-                nc.scalar.activation(
-                    grouped[:, gs].rearrange("p (c l t) -> p c t l", l=4, t=PACK),
-                    root[:, :, js].rearrange("p t (c l) -> p c t l", l=4),
-                    ACT.Square,
-                )
-                nc.vector.quantize_mx(codes[:, js].bitcast(FP8X4), scales[:, js], grouped[:, gs])
-            h_c[b] = codes
-            h_s[b] = scales
+        def square(root, grouped):
+            nc.scalar.activation(
+                grouped.rearrange("p (c l t) -> p c t l", l=4, t=PACK),
+                root.rearrange("p t (c l) -> p c t l", l=4),
+                ACT.Square,
+            )
+            return grouped
+
+        def quantise_h(b, half, grouped, slot):
+            codes = alloc("h_c%d%d" % (b, half), [P, HALF], U32, slot)
+            scales = alloc("h_s%d%d" % (b, half), [P, HALF], U8)
+            nc.vector.quantize_mx(codes[:].bitcast(FP8X4), scales[:], grouped)
+            h_c[(b, half)] = codes
+            h_s[(b, half)] = scales
 
         diff0 = [bank(t, "diff0%d" % t) for t in range(4)]
         diff1 = [bank(4 + t, "diff1%d" % t) for t in range(4)]
-        for t in range(4):
-            pocket_pass(diff0[t], 0, t, 0, True, False)
+        for a in range(2):
+            for g in range(8):
+                ligand_pass((diff0 + diff1)[g], g, a, a == 0, False)
         for a in range(2):
             for t in range(4):
-                ligand_pass(diff0[t], t, a, False, False)
-            for t in range(4):
-                ligand_pass(diff1[t], 4 + t, a, a == 0, False)
+                pocket_pass(diff0[t], 0, t, a, False, a == 1)
+        quantise_w2(1, 0, ())
         for t in range(4):
-            pocket_pass(diff0[t], 0, t, 1, False, True)
+            pocket_pass(diff1[t], 1, t, 0, False, False)
         root0 = make_root(0, diff0, 1)
-        for a in range(2):
-            quantise_w2(1, a, (0, 1) if a == 1 else ())
-            for t in range(4):
-                pocket_pass(diff1[t], 1, t, a, False, a == 1)
-        make_h(0, root0)
+        quantise_w2(1, 1, (3,))
+        for t in range(4):
+            pocket_pass(diff1[t], 1, t, 1, False, True)
+        h_g0 = alloc("h_g0", [P, PACK * S], BF16, "w2_raw11")
+        h_g1 = alloc("h_g1", [P, PACK * S], BF16)
+        h_g00 = square(root0[0], h_g0[:, 0 : PACK * HALF])
+        h_g01 = square(root0[1], h_g0[:, PACK * HALF : PACK * S])
+        w4_g0 = round_w4(0, nc.vector.tensor_copy, "w2_g11")
         root1 = make_root(1, diff1, 2)
-        quantise_w4(0)
-        quantise_w4(1)
-        make_h(1, root1)
+        w4_g1 = round_w4(1, nc.scalar.copy, None)
+        h_g10 = square(root1[0], h_g1[:, 0 : PACK * HALF])
+        h_g11 = square(root1[1], h_g1[:, PACK * HALF : PACK * S])
+        quantise_w4(0, w4_g0, "damp4")
+        quantise_h(0, 0, h_g00, "damp5")
+        quantise_h(0, 1, h_g01, "damp6")
+        quantise_w4(1, w4_g1, "damp7")
+        quantise_h(1, 0, h_g10, None)
+        quantise_h(1, 1, h_g11, None)
 
-        out_view = out.rearrange("(c p) j -> p c j", p=P)
         accs = [[bank(2 * half + i, "y%d%d" % (half, i)) for i in range(2)] for half in range(2)]
         for b in range(2):
             for half in range(2):
-                js = slice(half * HALF, (half + 1) * HALF)
                 for c in range(3):
                     ns = slice(c * P, (c + 1) * P)
                     nc.tensor.matmul_mx(
                         accs[half][c // 2][:, (c % 2) * HALF : (c % 2 + 1) * HALF],
                         lhsT=w4_c[b][:, ns].bitcast(FP8X4), lhsT_scale=w4_s[b][:, ns],
-                        rhs=h_c[b][:, js].bitcast(FP8X4), rhs_scale=h_s[b][:, js],
+                        rhs=h_c[(b, half)][:].bitcast(FP8X4), rhs_scale=h_s[(b, half)][:],
                         start=(b == 0 and c != 1), stop=(b == 1 and c != 0),
                     )
         for half in range(2):
             js = slice(half * HALF, (half + 1) * HALF)
-            result = alloc("result%d" % half, [P, 3, HALF], F32)
             for c in range(3):
+                result = alloc("result%d%d" % (half, c), [P, HALF], F32)
                 src = accs[half][c // 2][:, (c % 2) * HALF : (c % 2 + 1) * HALF]
-                if c == 2:
-                    nc.vector.tensor_scalar(result[:, c, :], src, cols[:, 8 + c : 9 + c], None, ALU.add)
+                if c == 2 and half == 1:
+                    nc.vector.tensor_scalar(result[:], src, bias_cols[:, c : c + 1], None, ALU.add)
                 else:
-                    nc.scalar.activation(result[:, c, :], src, ACT.Identity, bias=cols[:, 8 + c : 9 + c])
-            nc.sync.dma_start(out_view[:, :, js], result[:])
+                    nc.scalar.activation(result[:], src, ACT.Identity, bias=bias_cols[:, c : c + 1])
+                nc.sync.dma_start(out[c * P : (c + 1) * P, js], result[:])

@@ -80,13 +80,13 @@ def tile_list_solvent_docking_rescoring_kernel(
             )
             return ordered
 
-        tab3_plane = zeroed_plane(nc.gpsimd, "tab3_plane", T3)
-        w3_plane = zeroed_plane(nc.gpsimd, "w3_plane", H)
+        tab3_plane = zeroed_plane(nc.vector, "tab3_plane", T3)
+        w3_plane = zeroed_plane(nc.vector, "w3_plane", H)
         tab_plane = zeroed_plane(nc.vector, "tab_plane", 2 * T)
-        tab2_plane = zeroed_plane(nc.vector, "tab2_plane", T2)
         w1_plane = zeroed_plane(nc.vector, "w1_plane", 2 * H)
+        tab2_plane = zeroed_plane(nc.vector, "tab2_plane", T2)
 
-        rows = alloc("rows", [P, 2 * P], F32)
+        rows = alloc("rows", [P, 3 * P], F32)
         nc.gpsimd.memset(rows[:], 0.0)
         ident = alloc("ident", [P, P], F32)
         make_identity(nc, ident[:])
@@ -108,15 +108,15 @@ def tile_list_solvent_docking_rescoring_kernel(
                 nc.sync.dma_start(raw[:, t, :], src[t])
             w4_raw[b] = raw
 
+        nc.sync.dma_start(rows[0:4, 0 : 2 * P].rearrange("t (m l) -> t m l", l=4), gain.rearrange("(m t l) -> t m l", t=4, l=4))
+        nc.sync.dma_start(rows[4:5, :], bias.rearrange("(o n) -> o n", o=1))
         idx3 = load_list("idx3", offs3)
-        idx = load_list("idx", offs)
         tab3_w = load_words("tab3_w", tab3_words[0], T3, U16)
         w3_w = load_words("w3_w", w3_words[0].rearrange("p c i -> p (c i)"), H, U32)
         load_scale_rows(nc.sync, tab3_plane, tab3_scales)
         tab_w[0] = load_words("tab_w0", tab_words[0].rearrange("p c i -> p (c i)"), T, U32)
         load_scale_rows(nc.sync, w3_plane, w3_scales)
-        nc.sync.dma_start(rows[0:4, :].rearrange("t (m l) -> t m l", l=4), gain.rearrange("(m t l) -> t m l", t=4, l=4))
-        nc.sync.dma_start(rows[4:7, 0:P], bias.rearrange("(c p) -> c p", p=P))
+        idx = load_list("idx", offs)
         load_w2(0, 0)
         load_scale_rows(nc.sync, tab_plane, tab_scales)
         w1_w = alloc("w1_w", [P, 2 * 2 * H], U8)
@@ -139,13 +139,13 @@ def tile_list_solvent_docking_rescoring_kernel(
 
 
         turned = bank(7, "turned")
-        for b in range(2):
+        for b in range(3):
             nc.tensor.transpose(turned[:, b * P : (b + 1) * P], rows[:, b * P : (b + 1) * P], ident[:])
-        columns = turned[:, 0 : 2 * P].rearrange("p (b c) -> p b c", b=2)
+        columns = turned[:, 0 : 3 * P].rearrange("p (b c) -> p b c", b=3)
         root_gain = alloc("root_gain", [P, 2, 4], F32)
-        nc.scalar.activation(root_gain[:], columns[:, :, 0:4], ACT.Sqrt)
+        nc.scalar.activation(root_gain[:], columns[:, 0:2, 0:4], ACT.Sqrt)
         bias_cols = alloc("bias_cols", [P, 3], F32)
-        nc.scalar.copy(bias_cols[:], turned[:, 4:7])
+        nc.scalar.copy(bias_cols[:], columns[:, :, 4])
 
         v3_w = gather("v3_w", tab3_w[:], idx3, U16)
         w3_o = reorder("w3_o", w3_w, H, U32, 4)
@@ -165,7 +165,7 @@ def tile_list_solvent_docking_rescoring_kernel(
         w2_c = {}
         w2_s = {}
 
-        def quantise_w2(b, a, on_vector):
+        def quantise_w2(b, a, on_vector, slot=None):
             grouped = alloc("w2_g%d%d" % (b, a), [P, PACK * KP], BF16)
             src = w2_raw[(b, a)][:].rearrange("p j (m t l) -> p t m j l", t=4, l=4)
             dst = grouped[:].rearrange("p (t m l j) -> p t m j l", t=4, l=4, j=PACK)
@@ -174,7 +174,7 @@ def tile_list_solvent_docking_rescoring_kernel(
                     nc.vector.tensor_scalar(dst[:, t], src[:, t], -1.0, None, ALU.mult)
                 else:
                     nc.scalar.activation(dst[:, t], src[:, t], ACT.Copy, scale=-1.0)
-            codes = alloc("w2_c%d%d" % (b, a), [P, KP], U32)
+            codes = alloc("w2_c%d%d" % (b, a), [P, KP], U32, slot)
             scales = alloc("w2_s%d%d" % (b, a), [P, KP], U8)
             nc.vector.quantize_mx(codes[:].bitcast(FP8X4), scales[:], grouped[:])
             w2_c[(b, a)] = codes
@@ -182,16 +182,16 @@ def tile_list_solvent_docking_rescoring_kernel(
 
         v_w = [None, None]
         v_w[0] = gather("v_w0", tab_w[0][:], idx, U32)
-        w1_o = reorder("w1_o", w1_w, 2 * 2 * H, U8, 2)
         v_s = [gather("v_s%d" % a, tab_plane[:, a * T : (a + 1) * T], idx, U8) for a in range(2)]
+        w1_o = reorder("w1_o", w1_w, 2 * 2 * H, U8, 2)
         w1_s = reorder_plane("w1_s", w1_plane, 2 * H)
         v2_w = [None, None]
         v2_w[0] = gather("v2_w0", tab2_w[0][:], idx2, U32)
         v_w[1] = gather("v_w1", tab_w[1][:], idx, U32)
         v2_s = gather("v2_s", tab2_plane[:], idx2, U8)
-        quantise_w2(0, 0, ())
+        quantise_w2(0, 0, (), "tab2_plane")
         v2_w[1] = gather("v2_w1", tab2_w[1][:], idx2, U32)
-        quantise_w2(0, 1, ())
+        quantise_w2(0, 1, (), "tab2_w1")
 
         def ligand_pass(acc, g, a, start, stop):
             c0 = a * H + g * P
@@ -229,20 +229,18 @@ def tile_list_solvent_docking_rescoring_kernel(
         h_c = {}
         h_s = {}
 
-        def make_root(b, diff, pieces):
-            roots = []
+        def make_root(b, diff, pieces, slot):
             width = S // pieces
+            root = alloc("root%d" % b, [P, PACK * S], F32, slot)
+            view = root[:].rearrange("p (x t j) -> p x t j", x=pieces, t=PACK)
             for piece in range(pieces):
                 js = slice(piece * width, (piece + 1) * width)
-                root = alloc("root%d%d" % (b, piece), [P, PACK, width], F32)
                 for t in range(4):
-                    g = 4 * b + t
                     nc.vector.scalar_tensor_tensor(
-                        root[:, t, :], diff[t][:, js], root_gain[:, b, t : t + 1], damp[g][:, js], ALU.mult, ALU.mult
+                        view[:, piece, t, :], diff[t][:, js], root_gain[:, b, t : t + 1], damp[4 * b + t][:, js],
+                        ALU.mult, ALU.mult,
                     )
-                for j0 in range(0, width, HALF):
-                    roots.append(root[:, :, j0 : j0 + HALF])
-            return roots
+            return [view[:, j0 // width, :, j0 % width : j0 % width + HALF] for j0 in (0, HALF)]
 
         def square(root, grouped):
             nc.scalar.activation(
@@ -270,17 +268,17 @@ def tile_list_solvent_docking_rescoring_kernel(
         quantise_w2(1, 0, ())
         for t in range(4):
             pocket_pass(diff1[t], 1, t, 0, False, False)
-        root0 = make_root(0, diff0, 1)
+        root0 = make_root(0, diff0, 1, None)
         quantise_w2(1, 1, (3,))
         for t in range(4):
             pocket_pass(diff1[t], 1, t, 1, False, True)
         h_g0 = alloc("h_g0", [P, PACK * S], BF16, "w2_raw11")
-        h_g1 = alloc("h_g1", [P, PACK * S], BF16)
         h_g00 = square(root0[0], h_g0[:, 0 : PACK * HALF])
         h_g01 = square(root0[1], h_g0[:, PACK * HALF : PACK * S])
         w4_g0 = round_w4(0, nc.vector.tensor_copy, "w2_g11")
-        root1 = make_root(1, diff1, 2)
+        root1 = make_root(1, diff1, 2, "w4_raw0")
         w4_g1 = round_w4(1, nc.scalar.copy, None)
+        h_g1 = alloc("h_g1", [P, PACK * S], BF16, "w4_raw1")
         h_g10 = square(root1[0], h_g1[:, 0 : PACK * HALF])
         h_g11 = square(root1[1], h_g1[:, PACK * HALF : PACK * S])
         quantise_w4(0, w4_g0, "damp4")

@@ -21,6 +21,7 @@ P = 128
 PACK = 4
 KP = P * PACK
 HALF = S // 2
+TAB2_ROW = 8
 
 
 def tile_list_solvent_docking_rescoring_kernel(
@@ -54,6 +55,11 @@ def tile_list_solvent_docking_rescoring_kernel(
             for r in range(4):
                 queue.dma_start(plane[r:P:32, :].bitcast(I32).rearrange("q (a w) -> q a w", a=passes), rows[r])
 
+        def load_packed_rows(queue, plane, scales, row):
+            rows = scales.bitcast(I32)
+            for q in range(4):
+                queue.dma_start(plane[32 * q + row : 32 * q + row + 8, :].bitcast(I32), rows[:, 4 * q : 4 * q + 4, :])
+
         def load_words(name, src, width, dtype):
             words = alloc(name, [P, width], dtype)
             nc.sync.dma_start(words[:].bitcast(I32), src.bitcast(I32))
@@ -75,16 +81,16 @@ def tile_list_solvent_docking_rescoring_kernel(
         def reorder_plane(name, src, width):
             ordered = alloc(name, [P, width], U8)
             nc.vector.tensor_copy(
-                ordered[:].bitcast(I32).rearrange("p (g t m) -> p g t m", t=4, m=32),
-                src[:].bitcast(I32).rearrange("p (g m t) -> p g t m", t=4, m=32),
+                ordered[:].bitcast(I32).rearrange("p (g t x m) -> p g x t m", t=4, x=8, m=4),
+                src[:].bitcast(I32).rearrange("p (g x m t) -> p g x t m", t=4, x=8, m=4),
             )
             return ordered
 
         tab3_plane = zeroed_plane(nc.vector, "tab3_plane", T3)
         w3_plane = zeroed_plane(nc.vector, "w3_plane", H)
+        tab2_plane = zeroed_plane(nc.vector, "tab2_plane", T2)
         tab_plane = zeroed_plane(nc.vector, "tab_plane", 2 * T)
         w1_plane = zeroed_plane(nc.vector, "w1_plane", 2 * H)
-        tab2_plane = zeroed_plane(nc.vector, "tab2_plane", T2)
 
         rows = alloc("rows", [P, 3 * P], F32)
         nc.gpsimd.memset(rows[:], 0.0)
@@ -108,44 +114,32 @@ def tile_list_solvent_docking_rescoring_kernel(
                 nc.sync.dma_start(raw[:, t, :], src[t])
             w4_raw[b] = raw
 
-        nc.sync.dma_start(rows[0:4, 0 : 2 * P].rearrange("t (m l) -> t m l", l=4), gain.rearrange("(m t l) -> t m l", t=4, l=4))
-        nc.sync.dma_start(rows[4:5, :], bias.rearrange("(o n) -> o n", o=1))
         idx3 = load_list("idx3", offs3)
         tab3_w = load_words("tab3_w", tab3_words[0], T3, U16)
-        w3_w = load_words("w3_w", w3_words[0].rearrange("p c i -> p (c i)"), H, U32)
         load_scale_rows(nc.sync, tab3_plane, tab3_scales)
-        tab_w[0] = load_words("tab_w0", tab_words[0].rearrange("p c i -> p (c i)"), T, U32)
+        w3_w = load_words("w3_w", w3_words[0].rearrange("p c i -> p (c i)"), H, U32)
         load_scale_rows(nc.sync, w3_plane, w3_scales)
-        idx = load_list("idx", offs)
+        tab2_w[0] = load_words("tab2_w0", tab2_words[0].rearrange("p c i -> p (c i)"), T2, U32)
+        idx2 = load_list("idx2", offs2)
         load_w2(0, 0)
+        load_packed_rows(nc.sync, tab2_plane, tab2_scales, TAB2_ROW)
+        tab2_w[1] = load_words("tab2_w1", tab2_words[1].rearrange("p c i -> p (c i)"), T2, U32)
+        idx = load_list("idx", offs)
         load_scale_rows(nc.sync, tab_plane, tab_scales)
+        load_w2(0, 1)
         w1_w = alloc("w1_w", [P, 2 * 2 * H], U8)
         nc.sync.dma_start(
             w1_w[:].bitcast(I32).rearrange("p (a w) -> p a w", a=2), w1_words.bitcast(I32).rearrange("a p w -> p a w")
         )
-        tab2_w[0] = load_words("tab2_w0", tab2_words[0].rearrange("p c i -> p (c i)"), T2, U32)
         load_scale_rows(nc.sync, w1_plane, w1_scales)
-        idx2 = load_list("idx2", offs2)
+        nc.sync.dma_start(rows[0:4, 0 : 2 * P].rearrange("t (m l) -> t m l", l=4), gain.rearrange("(m t l) -> t m l", t=4, l=4))
+        nc.sync.dma_start(rows[4:5, :], bias.rearrange("(o n) -> o n", o=1))
+        tab_w[0] = load_words("tab_w0", tab_words[0].rearrange("p c i -> p (c i)"), T, U32)
         tab_w[1] = load_words("tab_w1", tab_words[1].rearrange("p c i -> p (c i)"), T, U32)
-        tab2_rows = tab2_scales.bitcast(I32)
-        for q in range(4):
-            nc.sync.dma_start(tab2_plane[32 * q + 4 : 32 * q + 12, :].bitcast(I32), tab2_rows[:, 4 * q : 4 * q + 4, :])
-        load_w2(0, 1)
-        tab2_w[1] = load_words("tab2_w1", tab2_words[1].rearrange("p c i -> p (c i)"), T2, U32)
         load_w2(1, 0)
         load_w2(1, 1)
         load_w4(0)
         load_w4(1)
-
-
-        turned = bank(7, "turned")
-        for b in range(3):
-            nc.tensor.transpose(turned[:, b * P : (b + 1) * P], rows[:, b * P : (b + 1) * P], ident[:])
-        columns = turned[:, 0 : 3 * P].rearrange("p (b c) -> p b c", b=3)
-        root_gain = alloc("root_gain", [P, 2, 4], F32)
-        nc.scalar.activation(root_gain[:], columns[:, 0:2, 0:4], ACT.Sqrt)
-        bias_cols = alloc("bias_cols", [P, 3], F32)
-        nc.scalar.copy(bias_cols[:], columns[:, :, 4])
 
         v3_w = gather("v3_w", tab3_w[:], idx3, U16)
         w3_o = reorder("w3_o", w3_w, H, U32, 4)
@@ -161,11 +155,21 @@ def tile_list_solvent_docking_rescoring_kernel(
             )
             nc.scalar.activation(damp[g][:], sol[:], ACT.Exp, scale=0.5)
 
+        turned = bank(7, "turned")
+        for b in range(3):
+            nc.tensor.transpose(turned[:, b * P : (b + 1) * P], rows[:, b * P : (b + 1) * P], ident[:])
+        columns = turned[:, 0 : 3 * P].rearrange("p (b c) -> p b c", b=3)
+        root_gain = alloc("root_gain", [P, 2, 4], F32)
+        nc.scalar.activation(root_gain[:], columns[:, 0:2, 0:4], ACT.Sqrt)
+        bias_cols = alloc("bias_cols", [P, 3], F32)
+        nc.scalar.copy(bias_cols[:], columns[:, :, 4])
 
         w2_c = {}
         w2_s = {}
 
-        def quantise_w2(b, a, on_vector, slot=None):
+        w2_g = {}
+
+        def round_w2(b, a, on_vector):
             grouped = alloc("w2_g%d%d" % (b, a), [P, PACK * KP], BF16)
             src = w2_raw[(b, a)][:].rearrange("p j (m t l) -> p t m j l", t=4, l=4)
             dst = grouped[:].rearrange("p (t m l j) -> p t m j l", t=4, l=4, j=PACK)
@@ -174,24 +178,34 @@ def tile_list_solvent_docking_rescoring_kernel(
                     nc.vector.tensor_scalar(dst[:, t], src[:, t], -1.0, None, ALU.mult)
                 else:
                     nc.scalar.activation(dst[:, t], src[:, t], ACT.Copy, scale=-1.0)
+            w2_g[(b, a)] = grouped
+
+        def quantise_w2(b, a, slot=None, pieces=1):
             codes = alloc("w2_c%d%d" % (b, a), [P, KP], U32, slot)
             scales = alloc("w2_s%d%d" % (b, a), [P, KP], U8)
-            nc.vector.quantize_mx(codes[:].bitcast(FP8X4), scales[:], grouped[:])
+            width = KP // pieces
+            for c in range(0, KP, width):
+                nc.vector.quantize_mx(
+                    codes[:, c : c + width].bitcast(FP8X4), scales[:, c : c + width],
+                    w2_g[(b, a)][:, PACK * c : PACK * (c + width)],
+                )
             w2_c[(b, a)] = codes
             w2_s[(b, a)] = scales
 
         v_w = [None, None]
-        v_w[0] = gather("v_w0", tab_w[0][:], idx, U32)
-        v_s = [gather("v_s%d" % a, tab_plane[:, a * T : (a + 1) * T], idx, U8) for a in range(2)]
-        w1_o = reorder("w1_o", w1_w, 2 * 2 * H, U8, 2)
-        w1_s = reorder_plane("w1_s", w1_plane, 2 * H)
         v2_w = [None, None]
         v2_w[0] = gather("v2_w0", tab2_w[0][:], idx2, U32)
-        v_w[1] = gather("v_w1", tab_w[1][:], idx, U32)
         v2_s = gather("v2_s", tab2_plane[:], idx2, U8)
-        quantise_w2(0, 0, (), "tab2_plane")
         v2_w[1] = gather("v2_w1", tab2_w[1][:], idx2, U32)
-        quantise_w2(0, 1, (), "tab2_w1")
+        v_s = [gather("v_s%d" % a, tab_plane[:, a * T : (a + 1) * T], idx, U8) for a in range(2)]
+        round_w2(0, 0, ())
+        quantise_w2(0, 0, "tab_plane")
+        w1_o = reorder("w1_o", w1_w, 2 * 2 * H, U8, 2)
+        w1_s = reorder_plane("w1_s", w1_plane, 2 * H)
+        round_w2(0, 1, ())
+        quantise_w2(0, 1, "w1_plane")
+        v_w[0] = gather("v_w0", tab_w[0][:], idx, U32)
+        v_w[1] = gather("v_w1", tab_w[1][:], idx, U32)
 
         def ligand_pass(acc, g, a, start, stop):
             c0 = a * H + g * P
@@ -204,43 +218,37 @@ def tile_list_solvent_docking_rescoring_kernel(
             cs = slice(t * P, (t + 1) * P)
             nc.tensor.matmul_mx(
                 acc[:], lhsT=w2_c[(b, a)][:, cs].bitcast(FP8X4), lhsT_scale=w2_s[(b, a)][:, cs],
-                rhs=v2_w[a][:].bitcast(FP8X4), rhs_scale=v2_s[4 + 4 * a : P, :], start=start, stop=stop,
+                rhs=v2_w[a][:].bitcast(FP8X4), rhs_scale=v2_s[TAB2_ROW + 4 * a : P, :], start=start, stop=stop,
             )
 
         w4_c = [None, None]
         w4_s = [None, None]
 
-        def round_w4(b, copy, slot):
+        def round_w4(b, shares, slot):
             grouped = alloc("w4_g%d" % b, [P, PACK * N], BF16, slot)
-            copy(
-                grouped[:].rearrange("p (c l t) -> p c t l", l=4, t=PACK),
-                w4_raw[b][:].rearrange("p t (c l) -> p c t l", l=4),
-            )
+            for copy, n0, n1 in shares:
+                copy(
+                    grouped[:, PACK * n0 : PACK * n1].rearrange("p (c l t) -> p c t l", l=4, t=PACK),
+                    w4_raw[b][:, :, n0:n1].rearrange("p t (c l) -> p c t l", l=4),
+                )
             return grouped
 
         def quantise_w4(b, grouped, slot):
             codes = alloc("w4_c%d" % b, [P, N], U32, slot)
             scales = alloc("w4_s%d" % b, [P, N], U8)
-            for c0, c1 in ((0, 256), (256, N)):
-                nc.vector.quantize_mx(codes[:, c0:c1].bitcast(FP8X4), scales[:, c0:c1], grouped[:, PACK * c0 : PACK * c1])
+            nc.vector.quantize_mx(codes[:].bitcast(FP8X4), scales[:], grouped[:])
             w4_c[b] = codes
             w4_s[b] = scales
 
         h_c = {}
         h_s = {}
 
-        def make_root(b, diff, pieces, slot):
-            width = S // pieces
-            root = alloc("root%d" % b, [P, PACK * S], F32, slot)
-            view = root[:].rearrange("p (x t j) -> p x t j", x=pieces, t=PACK)
-            for piece in range(pieces):
-                js = slice(piece * width, (piece + 1) * width)
-                for t in range(4):
-                    nc.vector.scalar_tensor_tensor(
-                        view[:, piece, t, :], diff[t][:, js], root_gain[:, b, t : t + 1], damp[4 * b + t][:, js],
-                        ALU.mult, ALU.mult,
-                    )
-            return [view[:, j0 // width, :, j0 % width : j0 % width + HALF] for j0 in (0, HALF)]
+        def make_root(b, half, diff, root):
+            js = slice(half * HALF, (half + 1) * HALF)
+            for t in range(4):
+                nc.vector.scalar_tensor_tensor(
+                    root[:, half, t, :], diff[t][:, js], root_gain[:, b, t : t + 1], damp[4 * b + t][:, js], ALU.mult, ALU.mult
+                )
 
         def square(root, grouped):
             nc.scalar.activation(
@@ -260,33 +268,42 @@ def tile_list_solvent_docking_rescoring_kernel(
         diff0 = [bank(t, "diff0%d" % t) for t in range(4)]
         diff1 = [bank(4 + t, "diff1%d" % t) for t in range(4)]
         for a in range(2):
-            for g in range(8):
-                ligand_pass((diff0 + diff1)[g], g, a, a == 0, False)
-        for a in range(2):
             for t in range(4):
-                pocket_pass(diff0[t], 0, t, a, False, a == 1)
-        quantise_w2(1, 0, ())
+                pocket_pass(diff0[t], 0, t, a, a == 0, False)
+        for t in range(4):
+            ligand_pass(diff0[t], t, 0, False, False)
+        for t in range(4):
+            ligand_pass(diff1[t], 4 + t, 0, True, False)
+        for t in range(4):
+            ligand_pass(diff0[t], t, 1, False, True)
+        for t in range(4):
+            ligand_pass(diff1[t], 4 + t, 1, False, False)
+        root0 = alloc("root0", [P, 2, PACK, HALF], F32)
+        root1 = alloc("root1", [P, 2, PACK, HALF], F32)
+        make_root(0, 0, diff0, root0)
+        make_root(0, 1, diff0, root0)
+        round_w2(1, 0, (3,))
+        quantise_w2(1, 0, None, 2)
         for t in range(4):
             pocket_pass(diff1[t], 1, t, 0, False, False)
-        root0 = make_root(0, diff0, 1, None)
-        quantise_w2(1, 1, (3,))
+        round_w2(1, 1, (0, 1, 2, 3))
+        quantise_w2(1, 1, None, 4)
         for t in range(4):
             pocket_pass(diff1[t], 1, t, 1, False, True)
-        h_g0 = alloc("h_g0", [P, PACK * S], BF16, "w2_raw11")
-        h_g00 = square(root0[0], h_g0[:, 0 : PACK * HALF])
-        h_g01 = square(root0[1], h_g0[:, PACK * HALF : PACK * S])
-        w4_g0 = round_w4(0, nc.vector.tensor_copy, "w2_g11")
-        root1 = make_root(1, diff1, 2, "w4_raw0")
-        w4_g1 = round_w4(1, nc.scalar.copy, None)
-        h_g1 = alloc("h_g1", [P, PACK * S], BF16, "w4_raw1")
-        h_g10 = square(root1[0], h_g1[:, 0 : PACK * HALF])
-        h_g11 = square(root1[1], h_g1[:, PACK * HALF : PACK * S])
-        quantise_w4(0, w4_g0, "damp4")
-        quantise_h(0, 0, h_g00, "damp5")
-        quantise_h(0, 1, h_g01, "damp6")
-        quantise_w4(1, w4_g1, "damp7")
-        quantise_h(1, 0, h_g10, None)
-        quantise_h(1, 1, h_g11, None)
+        h_g00 = square(root0[:, 0], alloc("h_g00", [P, PACK * HALF], BF16, "w2_raw10")[:])
+        h_g01 = square(root0[:, 1], alloc("h_g01", [P, PACK * HALF], BF16)[:])
+        make_root(1, 0, diff1, root1)
+        make_root(1, 1, diff1, root1)
+        w4_g0 = round_w4(0, ((nc.scalar.copy, 0, N),), None)
+        h_g10 = square(root1[:, 0], alloc("h_g10", [P, PACK * HALF], BF16, "w4_raw0")[:])
+        h_g11 = square(root1[:, 1], alloc("h_g11", [P, PACK * HALF], BF16)[:])
+        quantise_h(0, 0, h_g00, "w2_raw11")
+        quantise_w4(0, w4_g0, "damp7")
+        w4_g1 = round_w4(1, ((nc.vector.tensor_copy, 0, N),), "damp6")
+        quantise_h(1, 0, h_g10, "w4_raw1")
+        quantise_w4(1, w4_g1, None)
+        quantise_h(0, 1, h_g01, "damp5")
+        quantise_h(1, 1, h_g11, "damp6")
 
         accs = [[bank(2 * half + i, "y%d%d" % (half, i)) for i in range(2)] for half in range(2)]
         for b in range(2):
@@ -304,7 +321,7 @@ def tile_list_solvent_docking_rescoring_kernel(
             for c in range(3):
                 result = alloc("result%d%d" % (half, c), [P, HALF], F32)
                 src = accs[half][c // 2][:, (c % 2) * HALF : (c % 2 + 1) * HALF]
-                if c == 2 and half == 1:
+                if (c == 2) == (half == 0):
                     nc.vector.tensor_scalar(result[:], src, bias_cols[:, c : c + 1], None, ALU.add)
                 else:
                     nc.scalar.activation(result[:], src, ACT.Identity, bias=bias_cols[:, c : c + 1])

@@ -86,16 +86,14 @@ def tile_list_solvent_docking_rescoring_kernel(
             )
             return ordered
 
+        tab2_plane = zeroed_plane(nc.gpsimd, "tab2_plane", T2)
         tab3_plane = zeroed_plane(nc.vector, "tab3_plane", T3)
         w3_plane = zeroed_plane(nc.vector, "w3_plane", H)
-        tab2_plane = zeroed_plane(nc.vector, "tab2_plane", T2)
         tab_plane = zeroed_plane(nc.vector, "tab_plane", 2 * T)
         w1_plane = zeroed_plane(nc.vector, "w1_plane", 2 * H)
 
-        rows = alloc("rows", [P, 3 * P], F32)
+        rows = alloc("rows", [P, 4 * P], F32)
         nc.gpsimd.memset(rows[:], 0.0)
-        ident = alloc("ident", [P, P], F32)
-        make_identity(nc, ident[:])
 
         tab2_w = [None, None]
         tab_w = [None, None]
@@ -114,6 +112,15 @@ def tile_list_solvent_docking_rescoring_kernel(
                 nc.sync.dma_start(raw[:, t, :], src[t])
             w4_raw[b] = raw
 
+        load_packed_rows(nc.gpsimd, tab2_plane, tab2_scales, TAB2_ROW)
+        gain_rows = alloc("gain_rows", [2, KP], F32)
+        nc.gpsimd.dma_start(gain_rows[:], gain.rearrange("(b c) -> b c", b=2))
+        nc.gpsimd.dma_start(rows[2:3, 0:N], bias.rearrange("(o n) -> o n", o=1))
+        nc.gpsimd.tensor_copy(
+            rows[0:2, :].rearrange("b (t m l) -> b t m l", t=4, l=4), gain_rows[:].rearrange("b (m t l) -> b t m l", t=4, l=4)
+        )
+        ident = alloc("ident", [P, P], F32)
+        make_identity(nc, ident[:])
         idx3 = load_list("idx3", offs3)
         tab3_w = load_words("tab3_w", tab3_words[0], T3, U16)
         load_scale_rows(nc.sync, tab3_plane, tab3_scales)
@@ -122,7 +129,6 @@ def tile_list_solvent_docking_rescoring_kernel(
         tab2_w[0] = load_words("tab2_w0", tab2_words[0].rearrange("p c i -> p (c i)"), T2, U32)
         idx2 = load_list("idx2", offs2)
         load_w2(0, 0)
-        load_packed_rows(nc.sync, tab2_plane, tab2_scales, TAB2_ROW)
         tab2_w[1] = load_words("tab2_w1", tab2_words[1].rearrange("p c i -> p (c i)"), T2, U32)
         idx = load_list("idx", offs)
         load_scale_rows(nc.sync, tab_plane, tab_scales)
@@ -132,8 +138,6 @@ def tile_list_solvent_docking_rescoring_kernel(
             w1_w[:].bitcast(I32).rearrange("p (a w) -> p a w", a=2), w1_words.bitcast(I32).rearrange("a p w -> p a w")
         )
         load_scale_rows(nc.sync, w1_plane, w1_scales)
-        nc.sync.dma_start(rows[0:4, 0 : 2 * P].rearrange("t (m l) -> t m l", l=4), gain.rearrange("(m t l) -> t m l", t=4, l=4))
-        nc.sync.dma_start(rows[4:5, :], bias.rearrange("(o n) -> o n", o=1))
         tab_w[0] = load_words("tab_w0", tab_words[0].rearrange("p c i -> p (c i)"), T, U32)
         tab_w[1] = load_words("tab_w1", tab_words[1].rearrange("p c i -> p (c i)"), T, U32)
         load_w2(1, 0)
@@ -155,14 +159,6 @@ def tile_list_solvent_docking_rescoring_kernel(
             )
             nc.scalar.activation(damp[g][:], sol[:], ACT.Exp, scale=0.5)
 
-        turned = bank(7, "turned")
-        for b in range(3):
-            nc.tensor.transpose(turned[:, b * P : (b + 1) * P], rows[:, b * P : (b + 1) * P], ident[:])
-        columns = turned[:, 0 : 3 * P].rearrange("p (b c) -> p b c", b=3)
-        root_gain = alloc("root_gain", [P, 2, 4], F32)
-        nc.scalar.activation(root_gain[:], columns[:, 0:2, 0:4], ACT.Sqrt)
-        bias_cols = alloc("bias_cols", [P, 3], F32)
-        nc.scalar.copy(bias_cols[:], columns[:, :, 4])
 
         w2_c = {}
         w2_s = {}
@@ -195,15 +191,23 @@ def tile_list_solvent_docking_rescoring_kernel(
         v_w = [None, None]
         v2_w = [None, None]
         v2_w[0] = gather("v2_w0", tab2_w[0][:], idx2, U32)
-        v2_s = gather("v2_s", tab2_plane[:], idx2, U8)
         v2_w[1] = gather("v2_w1", tab2_w[1][:], idx2, U32)
         v_s = [gather("v_s%d" % a, tab_plane[:, a * T : (a + 1) * T], idx, U8) for a in range(2)]
+        v2_s = gather("v2_s", tab2_plane[:], idx2, U8, "tab_plane")
         round_w2(0, 0, ())
-        quantise_w2(0, 0, "tab_plane")
+        quantise_w2(0, 0, "tab2_plane")
         w1_o = reorder("w1_o", w1_w, 2 * 2 * H, U8, 2)
         w1_s = reorder_plane("w1_s", w1_plane, 2 * H)
         round_w2(0, 1, ())
         quantise_w2(0, 1, "w1_plane")
+        turned = bank(7, "turned")
+        for t in range(4):
+            nc.tensor.transpose(turned[:, t * P : (t + 1) * P], rows[:, t * P : (t + 1) * P], ident[:])
+        columns = turned[:].rearrange("p (t c) -> p t c", t=4)
+        root_gain = alloc("root_gain", [P, 4, 2], F32, "w2_raw01")
+        nc.scalar.activation(root_gain[:], columns[:, :, 0:2], ACT.Sqrt)
+        bias_cols = alloc("bias_cols", [P, 3], F32, "w2_g01")
+        nc.scalar.copy(bias_cols[:], columns[:, 0:3, 2])
         v_w[0] = gather("v_w0", tab_w[0][:], idx, U32)
         v_w[1] = gather("v_w1", tab_w[1][:], idx, U32)
 
@@ -247,7 +251,7 @@ def tile_list_solvent_docking_rescoring_kernel(
             js = slice(half * HALF, (half + 1) * HALF)
             for t in range(4):
                 nc.vector.scalar_tensor_tensor(
-                    root[:, half, t, :], diff[t][:, js], root_gain[:, b, t : t + 1], damp[4 * b + t][:, js], ALU.mult, ALU.mult
+                    root[:, half, t, :], diff[t][:, js], root_gain[:, t, b : b + 1], damp[4 * b + t][:, js], ALU.mult, ALU.mult
                 )
 
         def square(root, grouped):

@@ -78,24 +78,24 @@ def tile_list_solvent_docking_rescoring_kernel(
             )
             return ordered
 
-        def reorder_plane(name, src, width):
-            ordered = alloc(name, [P, width], U8)
+        def reorder_plane(name, src, width, slot=None):
+            ordered = alloc(name, [P, width], U8, slot)
             nc.vector.tensor_copy(
                 ordered[:].bitcast(I32).rearrange("p (g t x m) -> p g x t m", t=4, x=8, m=4),
                 src[:].bitcast(I32).rearrange("p (g x m t) -> p g x t m", t=4, x=8, m=4),
             )
             return ordered
 
-        tab2_plane = zeroed_plane(nc.gpsimd, "tab2_plane", T2)
         tab3_plane = zeroed_plane(nc.vector, "tab3_plane", T3)
-        w3_plane = zeroed_plane(nc.vector, "w3_plane", H)
         tab_plane = zeroed_plane(nc.vector, "tab_plane", 2 * T)
+        w3_plane = zeroed_plane(nc.vector, "w3_plane", H)
+        tab2_plane = zeroed_plane(nc.vector, "tab2_plane", T2)
         w1_plane = zeroed_plane(nc.vector, "w1_plane", 2 * H)
-
         rows = alloc("rows", [P, 4 * P], F32)
-        nc.gpsimd.memset(rows[:], 0.0)
+        nc.vector.memset(rows[:], 0.0)
+        ident = alloc("ident", [P, P], F32)
+        make_identity(nc, ident[:])
 
-        tab2_w = [None, None]
         tab_w = [None, None]
         w2_raw = {}
         w4_raw = [None, None]
@@ -112,33 +112,31 @@ def tile_list_solvent_docking_rescoring_kernel(
                 nc.sync.dma_start(raw[:, t, :], src[t])
             w4_raw[b] = raw
 
+        load_scale_rows(nc.gpsimd, tab_plane, tab_scales)
         load_packed_rows(nc.gpsimd, tab2_plane, tab2_scales, TAB2_ROW)
-        gain_rows = alloc("gain_rows", [2, KP], F32)
-        nc.gpsimd.dma_start(gain_rows[:], gain.rearrange("(b c) -> b c", b=2))
-        nc.gpsimd.dma_start(rows[2:3, 0:N], bias.rearrange("(o n) -> o n", o=1))
-        nc.gpsimd.tensor_copy(
-            rows[0:2, :].rearrange("b (t m l) -> b t m l", t=4, l=4), gain_rows[:].rearrange("b (m t l) -> b t m l", t=4, l=4)
-        )
-        ident = alloc("ident", [P, P], F32)
-        make_identity(nc, ident[:])
-        idx3 = load_list("idx3", offs3)
         tab3_w = load_words("tab3_w", tab3_words[0], T3, U16)
+        idx3 = load_list("idx3", offs3)
         load_scale_rows(nc.sync, tab3_plane, tab3_scales)
         w3_w = load_words("w3_w", w3_words[0].rearrange("p c i -> p (c i)"), H, U32)
         load_scale_rows(nc.sync, w3_plane, w3_scales)
-        tab2_w[0] = load_words("tab2_w0", tab2_words[0].rearrange("p c i -> p (c i)"), T2, U32)
-        idx2 = load_list("idx2", offs2)
-        load_w2(0, 0)
-        tab2_w[1] = load_words("tab2_w1", tab2_words[1].rearrange("p c i -> p (c i)"), T2, U32)
+        tab_w[0] = load_words("tab_w0", tab_words[0].rearrange("p c i -> p (c i)"), T, U32)
         idx = load_list("idx", offs)
-        load_scale_rows(nc.sync, tab_plane, tab_scales)
+        load_w2(0, 0)
         load_w2(0, 1)
+        gain_rows = alloc("gain_rows", [2, KP], F32)
+        nc.sync.dma_start(gain_rows[:], gain.rearrange("(b c) -> b c", b=2))
+        nc.sync.dma_start(rows[2:3, 0:N], bias.rearrange("(o n) -> o n", o=1))
         w1_w = alloc("w1_w", [P, 2 * 2 * H], U8)
         nc.sync.dma_start(
             w1_w[:].bitcast(I32).rearrange("p (a w) -> p a w", a=2), w1_words.bitcast(I32).rearrange("a p w -> p a w")
         )
         load_scale_rows(nc.sync, w1_plane, w1_scales)
-        tab_w[0] = load_words("tab_w0", tab_words[0].rearrange("p c i -> p (c i)"), T, U32)
+        idx2 = load_list("idx2", offs2)
+        tab2_w = alloc("tab2_w", [P, 2 * T2], U32)
+        nc.sync.dma_start(
+            tab2_w[:].bitcast(I32).rearrange("p (a w) -> p a w", a=2),
+            tab2_words.rearrange("a p c i -> p a (c i)").bitcast(I32),
+        )
         tab_w[1] = load_words("tab_w1", tab_words[1].rearrange("p c i -> p (c i)"), T, U32)
         load_w2(1, 0)
         load_w2(1, 1)
@@ -189,13 +187,13 @@ def tile_list_solvent_docking_rescoring_kernel(
             w2_s[(b, a)] = scales
 
         v_w = [None, None]
-        v2_w = [None, None]
-        v2_w[0] = gather("v2_w0", tab2_w[0][:], idx2, U32)
-        v2_w[1] = gather("v2_w1", tab2_w[1][:], idx2, U32)
-        v_s = [gather("v_s%d" % a, tab_plane[:, a * T : (a + 1) * T], idx, U8) for a in range(2)]
-        v2_s = gather("v2_s", tab2_plane[:], idx2, U8, "tab_plane")
+        v_w[0] = gather("v_w0", tab_w[0][:], idx, U32)
+        v_s = [gather("v_s%d" % a, tab_plane[:, a * T : (a + 1) * T], idx, U8, "tab_w0" if a == 0 else None) for a in range(2)]
         round_w2(0, 0, ())
-        quantise_w2(0, 0, "tab2_plane")
+        quantise_w2(0, 0, "tab_plane")
+        nc.vector.tensor_copy(
+            rows[0:2, :].rearrange("b (t m l) -> b t m l", t=4, l=4), gain_rows[:].rearrange("b (m t l) -> b t m l", t=4, l=4)
+        )
         w1_o = reorder("w1_o", w1_w, 2 * 2 * H, U8, 2)
         w1_s = reorder_plane("w1_s", w1_plane, 2 * H)
         round_w2(0, 1, ())
@@ -204,11 +202,12 @@ def tile_list_solvent_docking_rescoring_kernel(
         for t in range(4):
             nc.tensor.transpose(turned[:, t * P : (t + 1) * P], rows[:, t * P : (t + 1) * P], ident[:])
         columns = turned[:].rearrange("p (t c) -> p t c", t=4)
-        root_gain = alloc("root_gain", [P, 4, 2], F32, "w2_raw01")
+        root_gain = alloc("root_gain", [P, 4, 2], F32)
         nc.scalar.activation(root_gain[:], columns[:, :, 0:2], ACT.Sqrt)
-        bias_cols = alloc("bias_cols", [P, 3], F32, "w2_g01")
+        bias_cols = alloc("bias_cols", [P, 3], F32)
         nc.scalar.copy(bias_cols[:], columns[:, 0:3, 2])
-        v_w[0] = gather("v_w0", tab_w[0][:], idx, U32)
+        v2_s = gather("v2_s", tab2_plane[:], idx2, U8)
+        v2_w = [gather("v2_w%d" % a, tab2_w[:, a * T2 : (a + 1) * T2], idx2, U32) for a in range(2)]
         v_w[1] = gather("v_w1", tab_w[1][:], idx, U32)
 
         def ligand_pass(acc, g, a, start, stop):
@@ -271,13 +270,11 @@ def tile_list_solvent_docking_rescoring_kernel(
 
         diff0 = [bank(t, "diff0%d" % t) for t in range(4)]
         diff1 = [bank(4 + t, "diff1%d" % t) for t in range(4)]
+        for g in range(8):
+            ligand_pass((diff0 + diff1)[g], g, 0, True, False)
         for a in range(2):
             for t in range(4):
-                pocket_pass(diff0[t], 0, t, a, a == 0, False)
-        for t in range(4):
-            ligand_pass(diff0[t], t, 0, False, False)
-        for t in range(4):
-            ligand_pass(diff1[t], 4 + t, 0, True, False)
+                pocket_pass(diff0[t], 0, t, a, False, False)
         for t in range(4):
             ligand_pass(diff0[t], t, 1, False, True)
         for t in range(4):

@@ -121,8 +121,6 @@ def tile_list_solvent_docking_rescoring_kernel(
         load_scale_rows(nc.sync, w3_plane, w3_scales)
         tab_w[0] = load_words("tab_w0", tab_words[0].rearrange("p c i -> p (c i)"), T, U32)
         idx = load_list("idx", offs)
-        load_w2(0, 0)
-        load_w2(0, 1)
         gain_rows = alloc("gain_rows", [2, KP], F32)
         nc.sync.dma_start(gain_rows[:], gain.rearrange("(b c) -> b c", b=2))
         nc.sync.dma_start(rows[2:3, 0:N], bias.rearrange("(o n) -> o n", o=1))
@@ -131,12 +129,14 @@ def tile_list_solvent_docking_rescoring_kernel(
             w1_w[:].bitcast(I32).rearrange("p (a w) -> p a w", a=2), w1_words.bitcast(I32).rearrange("a p w -> p a w")
         )
         load_scale_rows(nc.sync, w1_plane, w1_scales)
-        idx2 = load_list("idx2", offs2)
         tab2_w = alloc("tab2_w", [P, 2 * T2], U32)
         nc.sync.dma_start(
             tab2_w[:].bitcast(I32).rearrange("p (a w) -> p a w", a=2),
             tab2_words.rearrange("a p c i -> p a (c i)").bitcast(I32),
         )
+        idx2 = load_list("idx2", offs2)
+        load_w2(0, 0)
+        load_w2(0, 1)
         tab_w[1] = load_words("tab_w1", tab_words[1].rearrange("p c i -> p (c i)"), T, U32)
         load_w2(1, 0)
         load_w2(1, 1)
@@ -189,15 +189,13 @@ def tile_list_solvent_docking_rescoring_kernel(
         v_w = [None, None]
         v_w[0] = gather("v_w0", tab_w[0][:], idx, U32)
         v_s = [gather("v_s%d" % a, tab_plane[:, a * T : (a + 1) * T], idx, U8, "tab_w0" if a == 0 else None) for a in range(2)]
-        round_w2(0, 0, ())
-        quantise_w2(0, 0, "tab_plane")
         nc.vector.tensor_copy(
             rows[0:2, :].rearrange("b (t m l) -> b t m l", t=4, l=4), gain_rows[:].rearrange("b (m t l) -> b t m l", t=4, l=4)
         )
         w1_o = reorder("w1_o", w1_w, 2 * 2 * H, U8, 2)
         w1_s = reorder_plane("w1_s", w1_plane, 2 * H)
-        round_w2(0, 1, ())
-        quantise_w2(0, 1, "w1_plane")
+        v2_w = [gather("v2_w%d" % a, tab2_w[:, a * T2 : (a + 1) * T2], idx2, U32) for a in range(2)]
+        v2_s = gather("v2_s", tab2_plane[:], idx2, U8, "tab2_w")
         turned = bank(7, "turned")
         for t in range(4):
             nc.tensor.transpose(turned[:, t * P : (t + 1) * P], rows[:, t * P : (t + 1) * P], ident[:])
@@ -206,8 +204,10 @@ def tile_list_solvent_docking_rescoring_kernel(
         nc.scalar.activation(root_gain[:], columns[:, :, 0:2], ACT.Sqrt)
         bias_cols = alloc("bias_cols", [P, 3], F32)
         nc.scalar.copy(bias_cols[:], columns[:, 0:3, 2])
-        v2_s = gather("v2_s", tab2_plane[:], idx2, U8)
-        v2_w = [gather("v2_w%d" % a, tab2_w[:, a * T2 : (a + 1) * T2], idx2, U32) for a in range(2)]
+        round_w2(0, 0, (0,))
+        quantise_w2(0, 0)
+        round_w2(0, 1, (0, 1))
+        quantise_w2(0, 1)
         v_w[1] = gather("v_w1", tab_w[1][:], idx, U32)
 
         def ligand_pass(acc, g, a, start, stop):
@@ -287,24 +287,24 @@ def tile_list_solvent_docking_rescoring_kernel(
         quantise_w2(1, 0, None, 2)
         for t in range(4):
             pocket_pass(diff1[t], 1, t, 0, False, False)
-        round_w2(1, 1, (0, 1, 2, 3))
+        h_g01 = square(root0[:, 1], alloc("h_g01", [P, PACK * HALF], BF16)[:])
+        round_w2(1, 1, (0, 1, 2))
+        quantise_h(0, 1, h_g01, "w2_g10")
         quantise_w2(1, 1, None, 4)
         for t in range(4):
             pocket_pass(diff1[t], 1, t, 1, False, True)
-        h_g00 = square(root0[:, 0], alloc("h_g00", [P, PACK * HALF], BF16, "w2_raw10")[:])
-        h_g01 = square(root0[:, 1], alloc("h_g01", [P, PACK * HALF], BF16)[:])
+        h_g00 = square(root0[:, 0], alloc("h_g00", [P, PACK * HALF], BF16, "w2_raw11")[:])
         make_root(1, 0, diff1, root1)
         make_root(1, 1, diff1, root1)
         w4_g0 = round_w4(0, ((nc.scalar.copy, 0, N),), None)
         h_g10 = square(root1[:, 0], alloc("h_g10", [P, PACK * HALF], BF16, "w4_raw0")[:])
         h_g11 = square(root1[:, 1], alloc("h_g11", [P, PACK * HALF], BF16)[:])
-        quantise_h(0, 0, h_g00, "w2_raw11")
-        quantise_w4(0, w4_g0, "damp7")
-        w4_g1 = round_w4(1, ((nc.vector.tensor_copy, 0, N),), "damp6")
-        quantise_h(1, 0, h_g10, "w4_raw1")
+        quantise_w4(0, w4_g0, "damp6")
+        quantise_h(0, 0, h_g00, "damp5")
+        w4_g1 = round_w4(1, ((nc.vector.tensor_copy, 0, N),), "damp7")
+        quantise_h(1, 0, h_g10, "damp4")
         quantise_w4(1, w4_g1, None)
-        quantise_h(0, 1, h_g01, "damp5")
-        quantise_h(1, 1, h_g11, "damp6")
+        quantise_h(1, 1, h_g11, None)
 
         accs = [[bank(2 * half + i, "y%d%d" % (half, i)) for i in range(2)] for half in range(2)]
         for b in range(2):

@@ -123,7 +123,7 @@ def tile_list_solvent_docking_rescoring_kernel(
         idx = load_list("idx", offs)
         gain_rows = alloc("gain_rows", [2, KP], F32)
         nc.sync.dma_start(gain_rows[:], gain.rearrange("(b c) -> b c", b=2))
-        nc.sync.dma_start(rows[2:3, 0:N], bias.rearrange("(o n) -> o n", o=1))
+        nc.sync.dma_start(rows[2:5, 0:P], bias.rearrange("(c n) -> c n", c=3))
         w1_w = alloc("w1_w", [P, 2 * 2 * H], U8)
         nc.sync.dma_start(
             w1_w[:].bitcast(I32).rearrange("p (a w) -> p a w", a=2), w1_words.bitcast(I32).rearrange("a p w -> p a w")
@@ -203,7 +203,7 @@ def tile_list_solvent_docking_rescoring_kernel(
         root_gain = alloc("root_gain", [P, 4, 2], F32)
         nc.scalar.activation(root_gain[:], columns[:, :, 0:2], ACT.Sqrt)
         bias_cols = alloc("bias_cols", [P, 3], F32)
-        nc.scalar.copy(bias_cols[:], columns[:, 0:3, 2])
+        nc.scalar.copy(bias_cols[:], columns[:, 0, 2:5])
         round_w2(0, 0, (0,))
         quantise_w2(0, 0)
         round_w2(0, 1, (0, 1))
@@ -306,24 +306,22 @@ def tile_list_solvent_docking_rescoring_kernel(
         quantise_w4(1, w4_g1, None)
         quantise_h(1, 1, h_g11, None)
 
-        accs = [[bank(2 * half + i, "y%d%d" % (half, i)) for i in range(2)] for half in range(2)]
+        accs = [[bank(3 * half + c, "y%d%d" % (half, c)) for c in range(3)] for half in range(2)]
         for b in range(2):
             for half in range(2):
                 for c in range(3):
                     ns = slice(c * P, (c + 1) * P)
                     nc.tensor.matmul_mx(
-                        accs[half][c // 2][:, (c % 2) * HALF : (c % 2 + 1) * HALF],
+                        accs[half][c][:, 0:HALF],
                         lhsT=w4_c[b][:, ns].bitcast(FP8X4), lhsT_scale=w4_s[b][:, ns],
                         rhs=h_c[(b, half)][:].bitcast(FP8X4), rhs_scale=h_s[(b, half)][:],
-                        start=(b == 0 and c != 1), stop=(b == 1 and c != 0),
+                        start=(b == 0), stop=(b == 1),
                     )
-        for half in range(2):
-            js = slice(half * HALF, (half + 1) * HALF)
-            for c in range(3):
-                result = alloc("result%d%d" % (half, c), [P, HALF], F32)
-                src = accs[half][c // 2][:, (c % 2) * HALF : (c % 2 + 1) * HALF]
-                if (c == 2) == (half == 0):
-                    nc.vector.tensor_scalar(result[:], src, bias_cols[:, c : c + 1], None, ALU.add)
-                else:
-                    nc.scalar.activation(result[:], src, ACT.Identity, bias=bias_cols[:, c : c + 1])
-                nc.sync.dma_start(out[c * P : (c + 1) * P, js], result[:])
+        for c in range(3):
+            result = alloc("result%d" % c, [P, S], F32)
+            nc.scalar.activation(result[:, 0:HALF], accs[0][c][:, 0:HALF], ACT.Identity, bias=bias_cols[:, c : c + 1])
+            if c == 0:
+                nc.sync.dma_start(out[0:P, 0:HALF], result[:, 0:HALF])
+            nc.vector.tensor_scalar(result[:, HALF:S], accs[1][c][:, 0:HALF], bias_cols[:, c : c + 1], None, ALU.add)
+            first = HALF if c == 0 else 0
+            nc.sync.dma_start(out[c * P : (c + 1) * P, first:S], result[:, first:S])

@@ -306,6 +306,9 @@ def tile_list_solvent_docking_rescoring_kernel(
         quantise_w4(1, w4_g1, None)
         quantise_h(1, 1, h_g11, None)
 
+        for t in range(4):
+            pocket_pass(bank(4 + t, "warm%d" % t), 1, t, 1, True, True)
+
         accs = [[bank(3 * half + c, "y%d%d" % (half, c)) for c in range(3)] for half in range(2)]
         for b in range(2):
             for half in range(2):

@@ -22,6 +22,8 @@ PACK = 4
 KP = P * PACK
 HALF = S // 2
 TAB2_ROW = 8
+TAB_ROW = 16
+LIVE_ROWS = 100
 
 
 def tile_list_solvent_docking_rescoring_kernel(
@@ -86,11 +88,20 @@ def tile_list_solvent_docking_rescoring_kernel(
             )
             return ordered
 
+        def deal_w1_plane(b, slot):
+            ordered = alloc("w1_s%d" % b, [P, H], U8, slot)
+            nc.vector.tensor_copy(
+                ordered[:].bitcast(I32).rearrange("p (a t x m) -> p a x t m", t=4, x=8, m=4),
+                w1_plane[:].bitcast(I32).rearrange("p (a g x m t) -> p g a x t m", g=2, t=4, x=8, m=4)[:, b],
+            )
+            return ordered
+
         tab3_plane = zeroed_plane(nc.vector, "tab3_plane", T3)
-        tab_plane = zeroed_plane(nc.vector, "tab_plane", 2 * T)
+        tab_plane = zeroed_plane(nc.vector, "tab_plane", T)
         w3_plane = zeroed_plane(nc.vector, "w3_plane", H)
         tab2_plane = zeroed_plane(nc.vector, "tab2_plane", T2)
         w1_plane = zeroed_plane(nc.vector, "w1_plane", 2 * H)
+        v_s = [zeroed_plane(nc.vector, "v_s%d" % a, S) for a in range(2)]
         rows = alloc("rows", [P, 4 * P], F32)
         nc.vector.memset(rows[:], 0.0)
         ident = alloc("ident", [P, P], F32)
@@ -105,6 +116,16 @@ def tile_list_solvent_docking_rescoring_kernel(
             nc.sync.dma_start(raw[:], w2[a * KP : (a + 1) * KP, b * KP : (b + 1) * KP].rearrange("(p j) c -> p j c", j=PACK))
             w2_raw[(b, a)] = raw
 
+        w1_w = [None, None]
+
+        def load_w1(b):
+            words = alloc("w1_w%d" % b, [P, 2 * H], U8)
+            nc.sync.dma_start(
+                words[:].bitcast(I32).rearrange("p (a w) -> p a w", a=2),
+                w1_words[:, :, b * H : (b + 1) * H].bitcast(I32).rearrange("a p w -> p a w"),
+            )
+            w1_w[b] = words
+
         def load_w4(b):
             raw = alloc("w4_raw%d" % b, [P, PACK, N], F32)
             src = w4[b * KP : (b + 1) * KP, :].rearrange("(m t l) n -> t m l n", t=4, l=4)
@@ -112,7 +133,7 @@ def tile_list_solvent_docking_rescoring_kernel(
                 nc.sync.dma_start(raw[:, t, :], src[t])
             w4_raw[b] = raw
 
-        load_scale_rows(nc.gpsimd, tab_plane, tab_scales)
+        load_packed_rows(nc.gpsimd, tab_plane, tab_scales, TAB_ROW)
         load_packed_rows(nc.gpsimd, tab2_plane, tab2_scales, TAB2_ROW)
         tab3_w = load_words("tab3_w", tab3_words[0], T3, U16)
         idx3 = load_list("idx3", offs3)
@@ -124,20 +145,18 @@ def tile_list_solvent_docking_rescoring_kernel(
         gain_rows = alloc("gain_rows", [2, KP], F32)
         nc.sync.dma_start(gain_rows[:], gain.rearrange("(b c) -> b c", b=2))
         nc.sync.dma_start(rows[2:5, 0:P], bias.rearrange("(c n) -> c n", c=3))
-        w1_w = alloc("w1_w", [P, 2 * 2 * H], U8)
-        nc.sync.dma_start(
-            w1_w[:].bitcast(I32).rearrange("p (a w) -> p a w", a=2), w1_words.bitcast(I32).rearrange("a p w -> p a w")
-        )
-        load_scale_rows(nc.sync, w1_plane, w1_scales)
         tab2_w = alloc("tab2_w", [P, 2 * T2], U32)
         nc.sync.dma_start(
             tab2_w[:].bitcast(I32).rearrange("p (a w) -> p a w", a=2),
             tab2_words.rearrange("a p c i -> p a (c i)").bitcast(I32),
         )
         idx2 = load_list("idx2", offs2)
+        load_w1(0)
+        load_scale_rows(nc.sync, w1_plane, w1_scales)
         load_w2(0, 0)
         load_w2(0, 1)
         tab_w[1] = load_words("tab_w1", tab_words[1].rearrange("p c i -> p (c i)"), T, U32)
+        load_w1(1)
         load_w2(1, 0)
         load_w2(1, 1)
         load_w4(0)
@@ -188,14 +207,17 @@ def tile_list_solvent_docking_rescoring_kernel(
 
         v_w = [None, None]
         v_w[0] = gather("v_w0", tab_w[0][:], idx, U32)
-        v_s = [gather("v_s%d" % a, tab_plane[:, a * T : (a + 1) * T], idx, U8, "tab_w0" if a == 0 else None) for a in range(2)]
+        v_packed = gather("v_packed", tab_plane[:], idx, U8, "tab_w0")
+        for a in range(2):
+            row = TAB_ROW + 4 * a
+            nc.gpsimd.dma_start(v_s[a][0:LIVE_ROWS, :].bitcast(I32), v_packed[row : row + LIVE_ROWS, :].bitcast(I32))
         nc.vector.tensor_copy(
             rows[0:2, :].rearrange("b (t m l) -> b t m l", t=4, l=4), gain_rows[:].rearrange("b (m t l) -> b t m l", t=4, l=4)
         )
-        w1_o = reorder("w1_o", w1_w, 2 * 2 * H, U8, 2)
-        w1_s = reorder_plane("w1_s", w1_plane, 2 * H)
         v2_w = [gather("v2_w%d" % a, tab2_w[:, a * T2 : (a + 1) * T2], idx2, U32) for a in range(2)]
         v2_s = gather("v2_s", tab2_plane[:], idx2, U8, "tab2_w")
+        w1_o = [reorder("w1_o0", w1_w[0], 2 * H, U8, 2), None]
+        w1_s = [deal_w1_plane(0, None), None]
         turned = bank(7, "turned")
         for t in range(4):
             nc.tensor.transpose(turned[:, t * P : (t + 1) * P], rows[:, t * P : (t + 1) * P], ident[:])
@@ -209,11 +231,13 @@ def tile_list_solvent_docking_rescoring_kernel(
         round_w2(0, 1, (0, 1))
         quantise_w2(0, 1)
         v_w[1] = gather("v_w1", tab_w[1][:], idx, U32)
+        w1_s[1] = deal_w1_plane(1, "tab_w1")
+        w1_o[1] = reorder("w1_o1", w1_w[1], 2 * H, U8, 2)
 
-        def ligand_pass(acc, g, a, start, stop):
-            c0 = a * H + g * P
+        def ligand_pass(acc, b, t, a, start, stop):
+            c0 = a * KP + t * P
             nc.tensor.matmul_mx(
-                acc[:], lhsT=w1_o[:, 2 * c0 : 2 * (c0 + P)].bitcast(FP4X4), lhsT_scale=w1_s[:, c0 : c0 + P],
+                acc[:], lhsT=w1_o[b][:, 2 * c0 : 2 * (c0 + P)].bitcast(FP4X4), lhsT_scale=w1_s[b][:, c0 : c0 + P],
                 rhs=v_w[a][:].bitcast(FP8X4), rhs_scale=v_s[a][:], start=start, stop=stop,
             )
 
@@ -270,19 +294,23 @@ def tile_list_solvent_docking_rescoring_kernel(
 
         diff0 = [bank(t, "diff0%d" % t) for t in range(4)]
         diff1 = [bank(4 + t, "diff1%d" % t) for t in range(4)]
-        for g in range(8):
-            ligand_pass((diff0 + diff1)[g], g, 0, True, False)
+        for t in range(4):
+            ligand_pass(diff0[t], 0, t, 0, True, False)
         for a in range(2):
             for t in range(4):
                 pocket_pass(diff0[t], 0, t, a, False, False)
         for t in range(4):
-            ligand_pass(diff0[t], t, 1, False, True)
-        for t in range(4):
-            ligand_pass(diff1[t], 4 + t, 1, False, False)
+            ligand_pass(diff0[t], 0, t, 1, False, True)
+        for a in range(2):
+            for t in range(4):
+                ligand_pass(diff1[t], 1, t, a, a == 0, False)
         root0 = alloc("root0", [P, 2, PACK, HALF], F32)
         root1 = alloc("root1", [P, 2, PACK, HALF], F32)
-        make_root(0, 0, diff0, root0)
-        make_root(0, 1, diff0, root0)
+        for t in range(4):
+            nc.vector.scalar_tensor_tensor(
+                root0[:, :, t, :], diff0[t][:].rearrange("p (h j) -> p h j", h=2), root_gain[:, t, 0:1],
+                damp[t][:].rearrange("p (h j) -> p h j", h=2), ALU.mult, ALU.mult,
+            )
         round_w2(1, 0, (3,))
         quantise_w2(1, 0, None, 2)
         for t in range(4):

@@ -12,6 +12,7 @@ I32 = mybir.dt.int32
 U32 = mybir.dt.uint32
 U16 = mybir.dt.uint16
 U8 = mybir.dt.uint8
+BYTES_OF = {F32: 4, BF16: 2, U32: 4, U16: 2, U8: 1}
 FP8X4 = mybir.dt.float8_e4m3fn_x4
 FP4X4 = mybir.dt.float4_e2m1fn_x4
 ACT = mybir.ActivationFunctionType
@@ -22,7 +23,7 @@ PACK = 4
 KP = P * PACK
 HALF = S // 2
 TAB2_ROW = 8
-TAB_ROW = 16
+TAB_ROW = 0
 LIVE_ROWS = 100
 
 
@@ -32,11 +33,22 @@ def tile_list_solvent_docking_rescoring_kernel(
 ):
     nc = tc.nc
     with ExitStack() as ctx:
+        lists = ctx.enter_context(tc.tile_pool(name="lists", bufs=1))
         sb = ctx.enter_context(tc.tile_pool(name="sb", bufs=1))
         psum = ctx.enter_context(tc.psum_pool(name="psum", bufs=1))
 
-        def alloc(name, shape, dtype, slot=None):
-            return sb.tile(shape, dtype, name=name, tag=slot or name, align_bytes=64)
+        places = {"end": 0}
+
+        def alloc(name, shape, dtype, slot=None, at=0):
+            if slot is None:
+                places[name] = places["end"]
+                size = BYTES_OF[dtype]
+                for extent in shape[1:]:
+                    size = size * extent
+                places["end"] = places[name] + (size + 63) // 64 * 64
+            else:
+                places[name] = places[slot] + at
+            return sb.tile(shape, dtype, name=name, align_bytes=64, offset=places[name])
 
         def bank(index, name):
             return psum.tile([P, S], F32, name=name, tag="bank%d" % index)
@@ -47,7 +59,7 @@ def tile_list_solvent_docking_rescoring_kernel(
             return plane
 
         def load_list(name, src):
-            offsets = sb.tile([P, S // 16], U16, name=name)
+            offsets = lists.tile([P, S // 16], U16, name=name)
             nc.sync.dma_start(offsets[:], src)
             return offsets
 
@@ -101,7 +113,7 @@ def tile_list_solvent_docking_rescoring_kernel(
         w3_plane = zeroed_plane(nc.vector, "w3_plane", H)
         tab2_plane = zeroed_plane(nc.vector, "tab2_plane", T2)
         w1_plane = zeroed_plane(nc.vector, "w1_plane", 2 * H)
-        v_s = [zeroed_plane(nc.vector, "v_s%d" % a, S) for a in range(2)]
+        v_moved = zeroed_plane(nc.vector, "v_moved", S)
         rows = alloc("rows", [P, 4 * P], F32)
         nc.vector.memset(rows[:], 0.0)
         ident = alloc("ident", [P, P], F32)
@@ -135,6 +147,7 @@ def tile_list_solvent_docking_rescoring_kernel(
 
         load_packed_rows(nc.gpsimd, tab_plane, tab_scales, TAB_ROW)
         load_packed_rows(nc.gpsimd, tab2_plane, tab2_scales, TAB2_ROW)
+        load_scale_rows(nc.gpsimd, w1_plane, w1_scales)
         tab3_w = load_words("tab3_w", tab3_words[0], T3, U16)
         idx3 = load_list("idx3", offs3)
         load_scale_rows(nc.sync, tab3_plane, tab3_scales)
@@ -144,7 +157,7 @@ def tile_list_solvent_docking_rescoring_kernel(
         idx = load_list("idx", offs)
         gain_rows = alloc("gain_rows", [2, KP], F32)
         nc.sync.dma_start(gain_rows[:], gain.rearrange("(b c) -> b c", b=2))
-        nc.sync.dma_start(rows[2:5, 0:P], bias.rearrange("(c n) -> c n", c=3))
+        nc.sync.dma_start(rows[2:3, 0:N], bias.rearrange("(c n) -> c n", c=1))
         tab2_w = alloc("tab2_w", [P, 2 * T2], U32)
         nc.sync.dma_start(
             tab2_w[:].bitcast(I32).rearrange("p (a w) -> p a w", a=2),
@@ -152,7 +165,6 @@ def tile_list_solvent_docking_rescoring_kernel(
         )
         idx2 = load_list("idx2", offs2)
         load_w1(0)
-        load_scale_rows(nc.sync, w1_plane, w1_scales)
         load_w2(0, 0)
         load_w2(0, 1)
         tab_w[1] = load_words("tab_w1", tab_words[1].rearrange("p c i -> p (c i)"), T, U32)
@@ -182,13 +194,18 @@ def tile_list_solvent_docking_rescoring_kernel(
 
         w2_g = {}
 
-        def round_w2(b, a, on_vector):
+        def round_w2(b, a, on_vector, on_gpsimd=()):
             grouped = alloc("w2_g%d%d" % (b, a), [P, PACK * KP], BF16)
             src = w2_raw[(b, a)][:].rearrange("p j (m t l) -> p t m j l", t=4, l=4)
             dst = grouped[:].rearrange("p (t m l j) -> p t m j l", t=4, l=4, j=PACK)
             for t in range(4):
                 if t in on_vector:
                     nc.vector.tensor_scalar(dst[:, t], src[:, t], -1.0, None, ALU.mult)
+                elif t in on_gpsimd:
+                    nc.gpsimd.tensor_scalar(
+                        dst[:, t].rearrange("p m j l -> p m l j"), src[:, t].rearrange("p m j l -> p m l j"),
+                        -1.0, 0.0, ALU.mult, ALU.add,
+                    )
                 else:
                     nc.scalar.activation(dst[:, t], src[:, t], ACT.Copy, scale=-1.0)
             w2_g[(b, a)] = grouped
@@ -208,16 +225,14 @@ def tile_list_solvent_docking_rescoring_kernel(
         v_w = [None, None]
         v_w[0] = gather("v_w0", tab_w[0][:], idx, U32)
         v_packed = gather("v_packed", tab_plane[:], idx, U8, "tab_w0")
-        for a in range(2):
-            row = TAB_ROW + 4 * a
-            nc.gpsimd.dma_start(v_s[a][0:LIVE_ROWS, :].bitcast(I32), v_packed[row : row + LIVE_ROWS, :].bitcast(I32))
+        nc.gpsimd.dma_start(v_moved[0:LIVE_ROWS, :].bitcast(I32), v_packed[4 : 4 + LIVE_ROWS, :].bitcast(I32))
+        v_s = [v_packed, v_moved]
         nc.vector.tensor_copy(
             rows[0:2, :].rearrange("b (t m l) -> b t m l", t=4, l=4), gain_rows[:].rearrange("b (m t l) -> b t m l", t=4, l=4)
         )
         v2_w = [gather("v2_w%d" % a, tab2_w[:, a * T2 : (a + 1) * T2], idx2, U32) for a in range(2)]
         v2_s = gather("v2_s", tab2_plane[:], idx2, U8, "tab2_w")
         w1_o = [reorder("w1_o0", w1_w[0], 2 * H, U8, 2), None]
-        w1_s = [deal_w1_plane(0, None), None]
         turned = bank(7, "turned")
         for t in range(4):
             nc.tensor.transpose(turned[:, t * P : (t + 1) * P], rows[:, t * P : (t + 1) * P], ident[:])
@@ -225,9 +240,10 @@ def tile_list_solvent_docking_rescoring_kernel(
         root_gain = alloc("root_gain", [P, 4, 2], F32)
         nc.scalar.activation(root_gain[:], columns[:, :, 0:2], ACT.Sqrt)
         bias_cols = alloc("bias_cols", [P, 3], F32)
-        nc.scalar.copy(bias_cols[:], columns[:, 0, 2:5])
+        nc.scalar.copy(bias_cols[:], columns[:, 0:3, 2])
         round_w2(0, 0, (0,))
         quantise_w2(0, 0)
+        w1_s = [deal_w1_plane(0, "tab2_plane"), None]
         round_w2(0, 1, (0, 1))
         quantise_w2(0, 1)
         v_w[1] = gather("v_w1", tab_w[1][:], idx, U32)
@@ -251,14 +267,14 @@ def tile_list_solvent_docking_rescoring_kernel(
         w4_c = [None, None]
         w4_s = [None, None]
 
-        def round_w4(b, shares, slot):
-            grouped = alloc("w4_g%d" % b, [P, PACK * N], BF16, slot)
-            for copy, n0, n1 in shares:
-                copy(
-                    grouped[:, PACK * n0 : PACK * n1].rearrange("p (c l t) -> p c t l", l=4, t=PACK),
-                    w4_raw[b][:, :, n0:n1].rearrange("p t (c l) -> p c t l", l=4),
-                )
-            return grouped
+        def round_w4(b, dst, c, copy):
+            src = w4_raw[b][:, :, c * P : (c + 1) * P]
+            copy(dst.rearrange("p (n l t) -> p n t l", l=4, t=PACK), src.rearrange("p t (n l) -> p n t l", l=4))
+
+        def gpsimd_round(dst, src):
+            nc.gpsimd.tensor_scalar(
+                dst.rearrange("p n t l -> p n l t"), src.rearrange("p n t l -> p n l t"), 1.0, 0.0, ALU.mult, ALU.add
+            )
 
         def quantise_w4(b, grouped, slot):
             codes = alloc("w4_c%d" % b, [P, N], U32, slot)
@@ -285,8 +301,8 @@ def tile_list_solvent_docking_rescoring_kernel(
             )
             return grouped
 
-        def quantise_h(b, half, grouped, slot):
-            codes = alloc("h_c%d%d" % (b, half), [P, HALF], U32, slot)
+        def quantise_h(b, half, grouped, slot, at=0):
+            codes = alloc("h_c%d%d" % (b, half), [P, HALF], U32, slot, at)
             scales = alloc("h_s%d%d" % (b, half), [P, HALF], U8)
             nc.vector.quantize_mx(codes[:].bitcast(FP8X4), scales[:], grouped)
             h_c[(b, half)] = codes
@@ -311,48 +327,68 @@ def tile_list_solvent_docking_rescoring_kernel(
                 root0[:, :, t, :], diff0[t][:].rearrange("p (h j) -> p h j", h=2), root_gain[:, t, 0:1],
                 damp[t][:].rearrange("p (h j) -> p h j", h=2), ALU.mult, ALU.mult,
             )
-        round_w2(1, 0, (3,))
+        round_w2(1, 0, (3,), (2,))
         quantise_w2(1, 0, None, 2)
         for t in range(4):
             pocket_pass(diff1[t], 1, t, 0, False, False)
-        h_g01 = square(root0[:, 1], alloc("h_g01", [P, PACK * HALF], BF16)[:])
+        h_g01 = square(root0[:, 1], alloc("h_g01", [P, PACK * HALF], BF16, "w2_raw10")[:])
         round_w2(1, 1, (0, 1, 2))
-        quantise_h(0, 1, h_g01, "w2_g10")
         quantise_w2(1, 1, None, 4)
         for t in range(4):
             pocket_pass(diff1[t], 1, t, 1, False, True)
         h_g00 = square(root0[:, 0], alloc("h_g00", [P, PACK * HALF], BF16, "w2_raw11")[:])
+        quantise_h(0, 1, h_g01, "w2_raw11", 2048)
         make_root(1, 0, diff1, root1)
         make_root(1, 1, diff1, root1)
-        w4_g0 = round_w4(0, ((nc.scalar.copy, 0, N),), None)
+        w4_g0 = alloc("w4_g0", [P, PACK * N], BF16, "w2_g11")
+        for c in range(3):
+            round_w4(0, w4_g0[:, c * KP : (c + 1) * KP], c, nc.scalar.copy if c == 0 else gpsimd_round)
         h_g10 = square(root1[:, 0], alloc("h_g10", [P, PACK * HALF], BF16, "w4_raw0")[:])
         h_g11 = square(root1[:, 1], alloc("h_g11", [P, PACK * HALF], BF16)[:])
-        quantise_w4(0, w4_g0, "damp6")
-        quantise_h(0, 0, h_g00, "damp5")
-        w4_g1 = round_w4(1, ((nc.vector.tensor_copy, 0, N),), "damp7")
-        quantise_h(1, 0, h_g10, "damp4")
-        quantise_w4(1, w4_g1, None)
-        quantise_h(1, 1, h_g11, None)
+        quantise_w4(0, w4_g0, "damp5")
+        quantise_h(0, 0, h_g00, "damp4")
+        w4_g1 = [alloc("w4_g1%d" % c, [P, PACK * P], BF16, "damp6", 2 * PACK * P * c) for c in range(3)]
+        w4_c[1] = alloc("w4_c1", [P, N], U32)
+        w4_s[1] = alloc("w4_s1", [P, N], U8)
+
+        def quantise_w4_tile(c):
+            ns = slice(c * P, (c + 1) * P)
+            nc.vector.quantize_mx(w4_c[1][:, ns].bitcast(FP8X4), w4_s[1][:, ns], w4_g1[c][:])
+
+        round_w4(1, w4_g1[0][:], 0, nc.vector.tensor_copy)
+        round_w4(1, w4_g1[1][:], 1, nc.vector.tensor_copy)
+        quantise_w4_tile(0)
+        quantise_h(1, 0, h_g10, "w4_g10")
+        round_w4(1, w4_g1[2][:], 2, nc.vector.tensor_copy)
+        quantise_w4_tile(1)
+        quantise_h(1, 1, h_g11, "w4_g11")
+        quantise_w4_tile(2)
 
         for t in range(4):
             pocket_pass(bank(4 + t, "warm%d" % t), 1, t, 1, True, True)
 
         accs = [[bank(3 * half + c, "y%d%d" % (half, c)) for c in range(3)] for half in range(2)]
-        for b in range(2):
-            for half in range(2):
-                for c in range(3):
-                    ns = slice(c * P, (c + 1) * P)
-                    nc.tensor.matmul_mx(
-                        accs[half][c][:, 0:HALF],
-                        lhsT=w4_c[b][:, ns].bitcast(FP8X4), lhsT_scale=w4_s[b][:, ns],
-                        rhs=h_c[(b, half)][:].bitcast(FP8X4), rhs_scale=h_s[(b, half)][:],
-                        start=(b == 0), stop=(b == 1),
-                    )
-        for c in range(3):
-            result = alloc("result%d" % c, [P, S], F32)
-            nc.scalar.activation(result[:, 0:HALF], accs[0][c][:, 0:HALF], ACT.Identity, bias=bias_cols[:, c : c + 1])
-            if c == 0:
-                nc.sync.dma_start(out[0:P, 0:HALF], result[:, 0:HALF])
-            nc.vector.tensor_scalar(result[:, HALF:S], accs[1][c][:, 0:HALF], bias_cols[:, c : c + 1], None, ALU.add)
-            first = HALF if c == 0 else 0
-            nc.sync.dma_start(out[c * P : (c + 1) * P, first:S], result[:, first:S])
+
+        def output_pass(b, half, c):
+            ns = slice(c * P, (c + 1) * P)
+            nc.tensor.matmul_mx(
+                accs[half][c][:, 0:HALF],
+                lhsT=w4_c[b][:, ns].bitcast(FP8X4), lhsT_scale=w4_s[b][:, ns],
+                rhs=h_c[(b, half)][:].bitcast(FP8X4), rhs_scale=h_s[(b, half)][:],
+                start=(b == 0), stop=(b == 1),
+            )
+
+        for half in range(2):
+            for c in range(3):
+                output_pass(0, half, c)
+        results = [alloc("result%d" % c, [P, S], F32) for c in range(3)]
+        for half, c in ((0, 0), (0, 1), (1, 0), (1, 1), (0, 2), (1, 2)):
+            output_pass(1, half, c)
+            js = slice(half * HALF, (half + 1) * HALF)
+            if half == 0:
+                nc.scalar.activation(results[c][:, js], accs[half][c][:, 0:HALF], ACT.Identity, bias=bias_cols[:, c : c + 1])
+            else:
+                nc.vector.tensor_scalar(results[c][:, js], accs[half][c][:, 0:HALF], bias_cols[:, c : c + 1], None, ALU.add)
+            if c < 2:
+                nc.sync.dma_start(out[c * P : (c + 1) * P, js], results[c][:, js])
+        nc.sync.dma_start(out[2 * P : 3 * P, :], results[2][:])

@@ -108,14 +108,14 @@ def tile_list_solvent_docking_rescoring_kernel(
             )
             return ordered
 
-        tab3_plane = zeroed_plane(nc.vector, "tab3_plane", T3)
         tab_plane = zeroed_plane(nc.vector, "tab_plane", T)
+        tab3_plane = zeroed_plane(nc.vector, "tab3_plane", T3)
+        rows = alloc("rows", [P, 4 * P], F32)
+        nc.vector.memset(rows[:], 0.0)
         w3_plane = zeroed_plane(nc.vector, "w3_plane", H)
         tab2_plane = zeroed_plane(nc.vector, "tab2_plane", T2)
         w1_plane = zeroed_plane(nc.vector, "w1_plane", 2 * H)
         v_moved = zeroed_plane(nc.vector, "v_moved", S)
-        rows = alloc("rows", [P, 4 * P], F32)
-        nc.vector.memset(rows[:], 0.0)
         ident = alloc("ident", [P, P], F32)
         make_identity(nc, ident[:])
 
@@ -147,17 +147,16 @@ def tile_list_solvent_docking_rescoring_kernel(
 
         load_packed_rows(nc.gpsimd, tab_plane, tab_scales, TAB_ROW)
         load_packed_rows(nc.gpsimd, tab2_plane, tab2_scales, TAB2_ROW)
-        load_scale_rows(nc.gpsimd, w1_plane, w1_scales)
         tab3_w = load_words("tab3_w", tab3_words[0], T3, U16)
+        gain_rows = alloc("gain_rows", [2, KP], F32)
+        nc.sync.dma_start(gain_rows[:], gain.rearrange("(b c) -> b c", b=2))
         idx3 = load_list("idx3", offs3)
         load_scale_rows(nc.sync, tab3_plane, tab3_scales)
         w3_w = load_words("w3_w", w3_words[0].rearrange("p c i -> p (c i)"), H, U32)
+        nc.sync.dma_start(rows[2:3, 0:N], bias.rearrange("(c n) -> c n", c=1))
         load_scale_rows(nc.sync, w3_plane, w3_scales)
         tab_w[0] = load_words("tab_w0", tab_words[0].rearrange("p c i -> p (c i)"), T, U32)
         idx = load_list("idx", offs)
-        gain_rows = alloc("gain_rows", [2, KP], F32)
-        nc.sync.dma_start(gain_rows[:], gain.rearrange("(b c) -> b c", b=2))
-        nc.sync.dma_start(rows[2:3, 0:N], bias.rearrange("(c n) -> c n", c=1))
         tab2_w = alloc("tab2_w", [P, 2 * T2], U32)
         nc.sync.dma_start(
             tab2_w[:].bitcast(I32).rearrange("p (a w) -> p a w", a=2),
@@ -165,6 +164,7 @@ def tile_list_solvent_docking_rescoring_kernel(
         )
         idx2 = load_list("idx2", offs2)
         load_w1(0)
+        load_scale_rows(nc.sync, w1_plane, w1_scales)
         load_w2(0, 0)
         load_w2(0, 1)
         tab_w[1] = load_words("tab_w1", tab_words[1].rearrange("p c i -> p (c i)"), T, U32)
@@ -173,6 +173,19 @@ def tile_list_solvent_docking_rescoring_kernel(
         load_w2(1, 1)
         load_w4(0)
         load_w4(1)
+
+        nc.scalar.activation(
+            rows[0:2, :].rearrange("b (t m l) -> b t m l", t=4, l=4),
+            gain_rows[:].rearrange("b (m t l) -> b t m l", t=4, l=4), ACT.Ln,
+        )
+        turned = bank(7, "turned")
+        for t in range(4):
+            nc.tensor.transpose(turned[:, t * P : (t + 1) * P], rows[:, t * P : (t + 1) * P], ident[:])
+        columns = turned[:].rearrange("p (t c) -> p t c", t=4)
+        half_log = alloc("half_log", [P, 4, 2], F32)
+        nc.scalar.activation(half_log[:], columns[:, :, 0:2], ACT.Copy, scale=0.5)
+        bias_cols = alloc("bias_cols", [P, 3], F32)
+        nc.scalar.copy(bias_cols[:], columns[:, 0:3, 2])
 
         v3_w = gather("v3_w", tab3_w[:], idx3, U16)
         w3_o = reorder("w3_o", w3_w, H, U32, 4)
@@ -186,7 +199,7 @@ def tile_list_solvent_docking_rescoring_kernel(
                 sol[:], lhsT=w3_o[:, cs].bitcast(FP8X4), lhsT_scale=w3_s[:, cs],
                 rhs=v3_w[:].bitcast(FP4X4), rhs_scale=v3_s[:], start=True, stop=True,
             )
-            nc.scalar.activation(damp[g][:], sol[:], ACT.Exp, scale=0.5)
+            nc.scalar.activation(damp[g][:], sol[:], ACT.Exp, bias=half_log[:, g % 4, g // 4 : g // 4 + 1], scale=0.5)
 
 
         w2_c = {}
@@ -227,23 +240,12 @@ def tile_list_solvent_docking_rescoring_kernel(
         v_packed = gather("v_packed", tab_plane[:], idx, U8, "tab_w0")
         nc.gpsimd.dma_start(v_moved[0:LIVE_ROWS, :].bitcast(I32), v_packed[4 : 4 + LIVE_ROWS, :].bitcast(I32))
         v_s = [v_packed, v_moved]
-        nc.vector.tensor_copy(
-            rows[0:2, :].rearrange("b (t m l) -> b t m l", t=4, l=4), gain_rows[:].rearrange("b (m t l) -> b t m l", t=4, l=4)
-        )
         v2_w = [gather("v2_w%d" % a, tab2_w[:, a * T2 : (a + 1) * T2], idx2, U32) for a in range(2)]
         v2_s = gather("v2_s", tab2_plane[:], idx2, U8, "tab2_w")
         w1_o = [reorder("w1_o0", w1_w[0], 2 * H, U8, 2), None]
-        turned = bank(7, "turned")
-        for t in range(4):
-            nc.tensor.transpose(turned[:, t * P : (t + 1) * P], rows[:, t * P : (t + 1) * P], ident[:])
-        columns = turned[:].rearrange("p (t c) -> p t c", t=4)
-        root_gain = alloc("root_gain", [P, 4, 2], F32)
-        nc.scalar.activation(root_gain[:], columns[:, :, 0:2], ACT.Sqrt)
-        bias_cols = alloc("bias_cols", [P, 3], F32)
-        nc.scalar.copy(bias_cols[:], columns[:, 0:3, 2])
         round_w2(0, 0, (0,))
         quantise_w2(0, 0)
-        w1_s = [deal_w1_plane(0, "tab2_plane"), None]
+        w1_s = [deal_w1_plane(0, None), None]
         round_w2(0, 1, (0, 1))
         quantise_w2(0, 1)
         v_w[1] = gather("v_w1", tab_w[1][:], idx, U32)
@@ -289,9 +291,7 @@ def tile_list_solvent_docking_rescoring_kernel(
         def make_root(b, half, diff, root):
             js = slice(half * HALF, (half + 1) * HALF)
             for t in range(4):
-                nc.vector.scalar_tensor_tensor(
-                    root[:, half, t, :], diff[t][:, js], root_gain[:, t, b : b + 1], damp[4 * b + t][:, js], ALU.mult, ALU.mult
-                )
+                nc.vector.tensor_tensor(root[:, half, t, :], diff[t][:, js], damp[4 * b + t][:, js], ALU.mult)
 
         def square(root, grouped):
             nc.scalar.activation(
@@ -323,9 +323,9 @@ def tile_list_solvent_docking_rescoring_kernel(
         root0 = alloc("root0", [P, 2, PACK, HALF], F32)
         root1 = alloc("root1", [P, 2, PACK, HALF], F32)
         for t in range(4):
-            nc.vector.scalar_tensor_tensor(
-                root0[:, :, t, :], diff0[t][:].rearrange("p (h j) -> p h j", h=2), root_gain[:, t, 0:1],
-                damp[t][:].rearrange("p (h j) -> p h j", h=2), ALU.mult, ALU.mult,
+            nc.vector.tensor_tensor(
+                root0[:, :, t, :], diff0[t][:].rearrange("p (h j) -> p h j", h=2),
+                damp[t][:].rearrange("p (h j) -> p h j", h=2), ALU.mult,
             )
         round_w2(1, 0, (3,), (2,))
         quantise_w2(1, 0, None, 2)

@@ -123,10 +123,14 @@ def tile_list_solvent_docking_rescoring_kernel(
         w2_raw = {}
         w4_raw = [None, None]
 
-        def load_w2(b, a):
-            raw = alloc("w2_raw%d%d" % (b, a), [P, PACK, KP], F32)
-            nc.sync.dma_start(raw[:], w2[a * KP : (a + 1) * KP, b * KP : (b + 1) * KP].rearrange("(p j) c -> p j c", j=PACK))
-            w2_raw[(b, a)] = raw
+        def load_w2(b, a, parts=1):
+            width = KP // parts
+            w2_raw[(b, a)] = []
+            for part in range(parts):
+                raw = alloc("w2_raw%d%d%d" % (b, a, part), [P, PACK, width], F32)
+                c0 = b * KP + part * width
+                nc.sync.dma_start(raw[:], w2[a * KP : (a + 1) * KP, c0 : c0 + width].rearrange("(p j) c -> p j c", j=PACK))
+                w2_raw[(b, a)].append(raw)
 
         w1_w = [None, None]
 
@@ -150,12 +154,12 @@ def tile_list_solvent_docking_rescoring_kernel(
         tab3_w = load_words("tab3_w", tab3_words[0], T3, U16)
         gain_rows = alloc("gain_rows", [2, KP], F32)
         nc.sync.dma_start(gain_rows[:], gain.rearrange("(b c) -> b c", b=2))
+        w3_w = load_words("w3_w", w3_words[0].rearrange("p c i -> p (c i)"), H, U32)
         idx3 = load_list("idx3", offs3)
         load_scale_rows(nc.sync, tab3_plane, tab3_scales)
-        w3_w = load_words("w3_w", w3_words[0].rearrange("p c i -> p (c i)"), H, U32)
         nc.sync.dma_start(rows[2:3, 0:N], bias.rearrange("(c n) -> c n", c=1))
-        load_scale_rows(nc.sync, w3_plane, w3_scales)
         tab_w[0] = load_words("tab_w0", tab_words[0].rearrange("p c i -> p (c i)"), T, U32)
+        load_scale_rows(nc.sync, w3_plane, w3_scales)
         idx = load_list("idx", offs)
         tab2_w = alloc("tab2_w", [P, 2 * T2], U32)
         nc.sync.dma_start(
@@ -169,8 +173,8 @@ def tile_list_solvent_docking_rescoring_kernel(
         load_w2(0, 1)
         tab_w[1] = load_words("tab_w1", tab_words[1].rearrange("p c i -> p (c i)"), T, U32)
         load_w1(1)
-        load_w2(1, 0)
-        load_w2(1, 1)
+        load_w2(1, 0, 2)
+        load_w2(1, 1, 2)
         load_w4(0)
         load_w4(1)
 
@@ -207,20 +211,23 @@ def tile_list_solvent_docking_rescoring_kernel(
 
         w2_g = {}
 
-        def round_w2(b, a, on_vector, on_gpsimd=()):
+        def round_w2(b, a, engines):
             grouped = alloc("w2_g%d%d" % (b, a), [P, PACK * KP], BF16)
-            src = w2_raw[(b, a)][:].rearrange("p j (m t l) -> p t m j l", t=4, l=4)
-            dst = grouped[:].rearrange("p (t m l j) -> p t m j l", t=4, l=4, j=PACK)
-            for t in range(4):
-                if t in on_vector:
-                    nc.vector.tensor_scalar(dst[:, t], src[:, t], -1.0, None, ALU.mult)
-                elif t in on_gpsimd:
-                    nc.gpsimd.tensor_scalar(
-                        dst[:, t].rearrange("p m j l -> p m l j"), src[:, t].rearrange("p m j l -> p m l j"),
-                        -1.0, 0.0, ALU.mult, ALU.add,
-                    )
-                else:
-                    nc.scalar.activation(dst[:, t], src[:, t], ACT.Copy, scale=-1.0)
+            parts = len(w2_raw[(b, a)])
+            for part in range(parts):
+                src = w2_raw[(b, a)][part][:].rearrange("p j (m t l) -> p t m j l", t=4, l=4)
+                dst = grouped[:].rearrange("p (t h m l j) -> p h t m j l", t=4, h=parts, l=4, j=PACK)[:, part]
+                for t in range(4):
+                    engine = engines[4 * part + t]
+                    if engine == "v":
+                        nc.vector.tensor_scalar(dst[:, t], src[:, t], -1.0, None, ALU.mult)
+                    elif engine == "g":
+                        nc.gpsimd.tensor_scalar(
+                            dst[:, t].rearrange("p m j l -> p m l j"), src[:, t].rearrange("p m j l -> p m l j"),
+                            -1.0, 0.0, ALU.mult, ALU.add,
+                        )
+                    else:
+                        nc.scalar.activation(dst[:, t], src[:, t], ACT.Copy, scale=-1.0)
             w2_g[(b, a)] = grouped
 
         def quantise_w2(b, a, slot=None, pieces=1):
@@ -243,10 +250,10 @@ def tile_list_solvent_docking_rescoring_kernel(
         v2_w = [gather("v2_w%d" % a, tab2_w[:, a * T2 : (a + 1) * T2], idx2, U32) for a in range(2)]
         v2_s = gather("v2_s", tab2_plane[:], idx2, U8, "tab2_w")
         w1_o = [reorder("w1_o0", w1_w[0], 2 * H, U8, 2), None]
-        round_w2(0, 0, (0,))
+        round_w2(0, 0, "vsss")
         quantise_w2(0, 0)
         w1_s = [deal_w1_plane(0, None), None]
-        round_w2(0, 1, (0, 1))
+        round_w2(0, 1, "vvss")
         quantise_w2(0, 1)
         v_w[1] = gather("v_w1", tab_w[1][:], idx, U32)
         w1_s[1] = deal_w1_plane(1, "tab_w1")
@@ -327,26 +334,27 @@ def tile_list_solvent_docking_rescoring_kernel(
                 root0[:, :, t, :], diff0[t][:].rearrange("p (h j) -> p h j", h=2),
                 damp[t][:].rearrange("p (h j) -> p h j", h=2), ALU.mult,
             )
-        round_w2(1, 0, (3,), (2,))
+        round_w2(1, 0, "sssssssg")
         quantise_w2(1, 0, None, 2)
         for t in range(4):
             pocket_pass(diff1[t], 1, t, 0, False, False)
-        h_g01 = square(root0[:, 1], alloc("h_g01", [P, PACK * HALF], BF16, "w2_raw10")[:])
-        round_w2(1, 1, (0, 1, 2))
+        h_g01 = square(root0[:, 1], alloc("h_g01", [P, PACK * HALF], BF16, "w2_raw101")[:])
+        round_w2(1, 1, "vvvvvvvs")
         quantise_w2(1, 1, None, 4)
         for t in range(4):
             pocket_pass(diff1[t], 1, t, 1, False, True)
-        h_g00 = square(root0[:, 0], alloc("h_g00", [P, PACK * HALF], BF16, "w2_raw11")[:])
-        quantise_h(0, 1, h_g01, "w2_raw11", 2048)
+        h_g00 = square(root0[:, 0], alloc("h_g00", [P, PACK * HALF], BF16, "w2_raw111")[:])
+        quantise_h(0, 1, h_g01, "w2_raw111", 2048)
         make_root(1, 0, diff1, root1)
         make_root(1, 1, diff1, root1)
         w4_g0 = alloc("w4_g0", [P, PACK * N], BF16, "w2_g11")
         for c in range(3):
-            round_w4(0, w4_g0[:, c * KP : (c + 1) * KP], c, nc.scalar.copy if c == 0 else gpsimd_round)
+            round_w4(0, w4_g0[:, c * KP : (c + 1) * KP], c, (nc.scalar.copy, nc.scalar.copy, gpsimd_round)[c])
         h_g10 = square(root1[:, 0], alloc("h_g10", [P, PACK * HALF], BF16, "w4_raw0")[:])
         h_g11 = square(root1[:, 1], alloc("h_g11", [P, PACK * HALF], BF16)[:])
         quantise_w4(0, w4_g0, "damp5")
         quantise_h(0, 0, h_g00, "damp4")
+        quantise_h(1, 0, h_g10, "h_g00")
         w4_g1 = [alloc("w4_g1%d" % c, [P, PACK * P], BF16, "damp6", 2 * PACK * P * c) for c in range(3)]
         w4_c[1] = alloc("w4_c1", [P, N], U32)
         w4_s[1] = alloc("w4_s1", [P, N], U8)
@@ -357,11 +365,10 @@ def tile_list_solvent_docking_rescoring_kernel(
 
         round_w4(1, w4_g1[0][:], 0, nc.vector.tensor_copy)
         round_w4(1, w4_g1[1][:], 1, nc.vector.tensor_copy)
+        round_w4(1, w4_g1[2][:], 2, nc.scalar.copy)
         quantise_w4_tile(0)
-        quantise_h(1, 0, h_g10, "w4_g10")
-        round_w4(1, w4_g1[2][:], 2, nc.vector.tensor_copy)
+        quantise_h(1, 1, h_g11, "w4_g10")
         quantise_w4_tile(1)
-        quantise_h(1, 1, h_g11, "w4_g11")
         quantise_w4_tile(2)
 
         for t in range(4):

@@ -100,14 +100,6 @@ def tile_list_solvent_docking_rescoring_kernel(
             )
             return ordered
 
-        def deal_w1_plane(b, slot):
-            ordered = alloc("w1_s%d" % b, [P, H], U8, slot)
-            nc.vector.tensor_copy(
-                ordered[:].bitcast(I32).rearrange("p (a t x m) -> p a x t m", t=4, x=8, m=4),
-                w1_plane[:].bitcast(I32).rearrange("p (a g x m t) -> p g a x t m", g=2, t=4, x=8, m=4)[:, b],
-            )
-            return ordered
-
         tab_plane = zeroed_plane(nc.vector, "tab_plane", T)
         tab3_plane = zeroed_plane(nc.vector, "tab3_plane", T3)
         rows = alloc("rows", [P, 4 * P], F32)
@@ -131,16 +123,6 @@ def tile_list_solvent_docking_rescoring_kernel(
                 c0 = b * KP + part * width
                 nc.sync.dma_start(raw[:], w2[a * KP : (a + 1) * KP, c0 : c0 + width].rearrange("(p j) c -> p j c", j=PACK))
                 w2_raw[(b, a)].append(raw)
-
-        w1_w = [None, None]
-
-        def load_w1(b):
-            words = alloc("w1_w%d" % b, [P, 2 * H], U8)
-            nc.sync.dma_start(
-                words[:].bitcast(I32).rearrange("p (a w) -> p a w", a=2),
-                w1_words[:, :, b * H : (b + 1) * H].bitcast(I32).rearrange("a p w -> p a w"),
-            )
-            w1_w[b] = words
 
         def load_w4(b):
             raw = alloc("w4_raw%d" % b, [P, PACK, N], F32)
@@ -167,14 +149,16 @@ def tile_list_solvent_docking_rescoring_kernel(
             tab2_words.rearrange("a p c i -> p a (c i)").bitcast(I32),
         )
         idx2 = load_list("idx2", offs2)
-        load_w1(0)
+        w1_w = alloc("w1_w", [P, 2 * 2 * H], U8)
+        nc.sync.dma_start(
+            w1_w[:].bitcast(I32).rearrange("p (a w) -> p a w", a=2), w1_words.bitcast(I32).rearrange("a p w -> p a w")
+        )
         load_scale_rows(nc.sync, w1_plane, w1_scales)
         load_w2(0, 0)
         load_w2(0, 1)
         tab_w[1] = load_words("tab_w1", tab_words[1].rearrange("p c i -> p (c i)"), T, U32)
-        load_w1(1)
-        load_w2(1, 0, 2)
-        load_w2(1, 1, 2)
+        load_w2(1, 0)
+        load_w2(1, 1)
         load_w4(0)
         load_w4(1)
 
@@ -195,7 +179,7 @@ def tile_list_solvent_docking_rescoring_kernel(
         w3_o = reorder("w3_o", w3_w, H, U32, 4)
         v3_s = gather("v3_s", tab3_plane[:], idx3, U8)
         w3_s = reorder_plane("w3_s", w3_plane, H)
-        damp = [alloc("damp%d" % g, [P, S], F32) for g in range(8)]
+        damp = [alloc("damp%d" % pair, [P, 2, S], F32) for pair in range(4)]
         for g in range(8):
             cs = slice(g * P, (g + 1) * P)
             sol = bank(g, "sol%d" % g)
@@ -203,7 +187,7 @@ def tile_list_solvent_docking_rescoring_kernel(
                 sol[:], lhsT=w3_o[:, cs].bitcast(FP8X4), lhsT_scale=w3_s[:, cs],
                 rhs=v3_w[:].bitcast(FP4X4), rhs_scale=v3_s[:], start=True, stop=True,
             )
-            nc.scalar.activation(damp[g][:], sol[:], ACT.Exp, bias=half_log[:, g % 4, g // 4 : g // 4 + 1], scale=0.5)
+            nc.scalar.activation(damp[g // 2][:, g % 2, :], sol[:], ACT.Exp, bias=half_log[:, g % 4, g // 4 : g // 4 + 1], scale=0.5)
 
 
         w2_c = {}
@@ -211,36 +195,30 @@ def tile_list_solvent_docking_rescoring_kernel(
 
         w2_g = {}
 
-        def round_w2(b, a, engines):
-            grouped = alloc("w2_g%d%d" % (b, a), [P, PACK * KP], BF16)
-            parts = len(w2_raw[(b, a)])
-            for part in range(parts):
-                src = w2_raw[(b, a)][part][:].rearrange("p j (m t l) -> p t m j l", t=4, l=4)
-                dst = grouped[:].rearrange("p (t h m l j) -> p h t m j l", t=4, h=parts, l=4, j=PACK)[:, part]
-                for t in range(4):
-                    engine = engines[4 * part + t]
-                    if engine == "v":
-                        nc.vector.tensor_scalar(dst[:, t], src[:, t], -1.0, None, ALU.mult)
-                    elif engine == "g":
-                        nc.gpsimd.tensor_scalar(
-                            dst[:, t].rearrange("p m j l -> p m l j"), src[:, t].rearrange("p m j l -> p m l j"),
-                            -1.0, 0.0, ALU.mult, ALU.add,
-                        )
-                    else:
-                        nc.scalar.activation(dst[:, t], src[:, t], ACT.Copy, scale=-1.0)
+        def round_w2(b, a, engines, pieces=1):
+            width = PACK * KP // pieces
+            grouped = [alloc("w2_g%d%d%d" % (b, a, i), [P, width], BF16) for i in range(pieces)]
+            src = w2_raw[(b, a)][0][:].rearrange("p j (m t l) -> p t m j l", t=4, l=4)
+            for t in range(4):
+                c0 = t * KP % width
+                dst = grouped[t * KP // width][:, c0 : c0 + KP].rearrange("p (m l j) -> p m j l", l=4, j=PACK)
+                if engines[t] == "v":
+                    nc.vector.tensor_scalar(dst, src[:, t], -1.0, None, ALU.mult)
+                elif engines[t] == "g":
+                    nc.gpsimd.tensor_scalar(
+                        dst.rearrange("p m j l -> p m l j"), src[:, t].rearrange("p m j l -> p m l j"),
+                        -1.0, 0.0, ALU.mult, ALU.add,
+                    )
+                else:
+                    nc.scalar.activation(dst, src[:, t], ACT.Copy, scale=-1.0)
             w2_g[(b, a)] = grouped
+            w2_c[(b, a)] = alloc("w2_c%d%d" % (b, a), [P, KP], U32)
+            w2_s[(b, a)] = alloc("w2_s%d%d" % (b, a), [P, KP], U8)
 
-        def quantise_w2(b, a, slot=None, pieces=1):
-            codes = alloc("w2_c%d%d" % (b, a), [P, KP], U32, slot)
-            scales = alloc("w2_s%d%d" % (b, a), [P, KP], U8)
-            width = KP // pieces
-            for c in range(0, KP, width):
-                nc.vector.quantize_mx(
-                    codes[:, c : c + width].bitcast(FP8X4), scales[:, c : c + width],
-                    w2_g[(b, a)][:, PACK * c : PACK * (c + width)],
-                )
-            w2_c[(b, a)] = codes
-            w2_s[(b, a)] = scales
+        def quantise_w2(b, a, piece=0):
+            width = KP // len(w2_g[(b, a)])
+            cs = slice(piece * width, (piece + 1) * width)
+            nc.vector.quantize_mx(w2_c[(b, a)][:, cs].bitcast(FP8X4), w2_s[(b, a)][:, cs], w2_g[(b, a)][piece][:])
 
         v_w = [None, None]
         v_w[0] = gather("v_w0", tab_w[0][:], idx, U32)
@@ -249,28 +227,30 @@ def tile_list_solvent_docking_rescoring_kernel(
         v_s = [v_packed, v_moved]
         v2_w = [gather("v2_w%d" % a, tab2_w[:, a * T2 : (a + 1) * T2], idx2, U32) for a in range(2)]
         v2_s = gather("v2_s", tab2_plane[:], idx2, U8, "tab2_w")
-        w1_o = [reorder("w1_o0", w1_w[0], 2 * H, U8, 2), None]
+        w1_o = reorder("w1_o", w1_w, 2 * 2 * H, U8, 2)
+        w1_s = reorder_plane("w1_s", w1_plane, 2 * H)
         round_w2(0, 0, "vsss")
         quantise_w2(0, 0)
-        w1_s = [deal_w1_plane(0, None), None]
-        round_w2(0, 1, "vvss")
-        quantise_w2(0, 1)
-        v_w[1] = gather("v_w1", tab_w[1][:], idx, U32)
-        w1_s[1] = deal_w1_plane(1, "tab_w1")
-        w1_o[1] = reorder("w1_o1", w1_w[1], 2 * H, U8, 2)
+        round_w2(0, 1, "vvss", 2)
+        quantise_w2(0, 1, 0)
+        quantise_w2(0, 1, 1)
+        v_w[1] = alloc("v_w1", [P, S], U32)
+        halves = [slice(half * HALF, (half + 1) * HALF) for half in range(2)]
+        for half in range(2):
+            nc.vector.tensor_copy(v_w[1][:, halves[half]], tab_w[1][:].indirect(idx[:, 16 * half : 16 * (half + 1)]))
 
-        def ligand_pass(acc, b, t, a, start, stop):
-            c0 = a * KP + t * P
+        def ligand_pass(acc, b, t, a, js, start, stop):
+            c0 = a * H + b * KP + t * P
             nc.tensor.matmul_mx(
-                acc[:], lhsT=w1_o[b][:, 2 * c0 : 2 * (c0 + P)].bitcast(FP4X4), lhsT_scale=w1_s[b][:, c0 : c0 + P],
-                rhs=v_w[a][:].bitcast(FP8X4), rhs_scale=v_s[a][:], start=start, stop=stop,
+                acc, lhsT=w1_o[:, 2 * c0 : 2 * (c0 + P)].bitcast(FP4X4), lhsT_scale=w1_s[:, c0 : c0 + P],
+                rhs=v_w[a][:, js].bitcast(FP8X4), rhs_scale=v_s[a][:, js], start=start, stop=stop,
             )
 
-        def pocket_pass(acc, b, t, a, start, stop):
+        def pocket_pass(acc, b, t, a, js, start, stop):
             cs = slice(t * P, (t + 1) * P)
             nc.tensor.matmul_mx(
-                acc[:], lhsT=w2_c[(b, a)][:, cs].bitcast(FP8X4), lhsT_scale=w2_s[(b, a)][:, cs],
-                rhs=v2_w[a][:].bitcast(FP8X4), rhs_scale=v2_s[TAB2_ROW + 4 * a : P, :], start=start, stop=stop,
+                acc, lhsT=w2_c[(b, a)][:, cs].bitcast(FP8X4), lhsT_scale=w2_s[(b, a)][:, cs],
+                rhs=v2_w[a][:, js].bitcast(FP8X4), rhs_scale=v2_s[TAB2_ROW + 4 * a : P, js], start=start, stop=stop,
             )
 
         w4_c = [None, None]
@@ -298,7 +278,7 @@ def tile_list_solvent_docking_rescoring_kernel(
         def make_root(b, half, diff, root):
             js = slice(half * HALF, (half + 1) * HALF)
             for t in range(4):
-                nc.vector.tensor_tensor(root[:, half, t, :], diff[t][:, js], damp[4 * b + t][:, js], ALU.mult)
+                nc.vector.tensor_tensor(root[:, half, t, :], diff[t][:, js], damp[2 * b + t // 2][:, t % 2, js], ALU.mult)
 
         def square(root, grouped):
             nc.scalar.activation(
@@ -315,47 +295,62 @@ def tile_list_solvent_docking_rescoring_kernel(
             h_c[(b, half)] = codes
             h_s[(b, half)] = scales
 
-        diff0 = [bank(t, "diff0%d" % t) for t in range(4)]
+        every = slice(0, S)
+        diff0 = [[bank(2 * half + pair, "diff0%d%d" % (half, pair)) for pair in range(2)] for half in range(2)]
         diff1 = [bank(4 + t, "diff1%d" % t) for t in range(4)]
-        for t in range(4):
-            ligand_pass(diff0[t], 0, t, 0, True, False)
-        for a in range(2):
+
+        def first_group(one_pass, a, start, stop):
+            for half in range(2):
+                for t in range(4):
+                    acc = diff0[half][t // 2][:, halves[t % 2]]
+                    one_pass(acc, 0, t, a, halves[half], start and t % 2 == 0, stop and t % 2 == 1)
+
+        first_group(ligand_pass, 0, True, False)
+        first_group(pocket_pass, 0, False, False)
+        first_group(pocket_pass, 1, False, False)
+        first_group(ligand_pass, 1, False, True)
+        for a in (1, 0):
             for t in range(4):
-                pocket_pass(diff0[t], 0, t, a, False, False)
-        for t in range(4):
-            ligand_pass(diff0[t], 0, t, 1, False, True)
-        for a in range(2):
-            for t in range(4):
-                ligand_pass(diff1[t], 1, t, a, a == 0, False)
+                ligand_pass(diff1[t][:], 1, t, a, every, a == 1, False)
         root0 = alloc("root0", [P, 2, PACK, HALF], F32)
         root1 = alloc("root1", [P, 2, PACK, HALF], F32)
+        for half in range(2):
+            for pair in range(2):
+                nc.vector.tensor_tensor(
+                    root0[:, half, 2 * pair : 2 * pair + 2, :], diff0[half][pair][:].rearrange("p (t j) -> p t j", t=2),
+                    damp[pair][:, :, halves[half]], ALU.mult,
+                )
+        h_g00 = square(root0[:, 0], alloc("h_g00", [P, PACK * HALF], BF16)[:])
+        h_g01 = square(root0[:, 1], alloc("h_g01", [P, PACK * HALF], BF16)[:])
+        round_w2(1, 0, "vvgv", 2)
+        for piece in (1, 0):
+            quantise_w2(1, 0, piece)
+        for t in (2, 3, 0, 1):
+            pocket_pass(diff1[t][:], 1, t, 0, every, False, False)
+        round_w2(1, 1, "vvss", 4)
+        quantise_w2(1, 1, 0)
+        quantise_w2(1, 1, 1)
+        quantise_w2(1, 1, 2)
+        quantise_h(0, 0, h_g00, "w2_g110")
+        quantise_w2(1, 1, 3)
+        quantise_h(0, 1, h_g01, "w2_g112")
         for t in range(4):
-            nc.vector.tensor_tensor(
-                root0[:, :, t, :], diff0[t][:].rearrange("p (h j) -> p h j", h=2),
-                damp[t][:].rearrange("p (h j) -> p h j", h=2), ALU.mult,
-            )
-        round_w2(1, 0, "sssssssg")
-        quantise_w2(1, 0, None, 2)
-        for t in range(4):
-            pocket_pass(diff1[t], 1, t, 0, False, False)
-        h_g01 = square(root0[:, 1], alloc("h_g01", [P, PACK * HALF], BF16, "w2_raw101")[:])
-        round_w2(1, 1, "vvvvvvvs")
-        quantise_w2(1, 1, None, 4)
-        for t in range(4):
-            pocket_pass(diff1[t], 1, t, 1, False, True)
-        h_g00 = square(root0[:, 0], alloc("h_g00", [P, PACK * HALF], BF16, "w2_raw111")[:])
-        quantise_h(0, 1, h_g01, "w2_raw111", 2048)
+            pocket_pass(diff1[t][:], 1, t, 1, every, False, True)
         make_root(1, 0, diff1, root1)
         make_root(1, 1, diff1, root1)
-        w4_g0 = alloc("w4_g0", [P, PACK * N], BF16, "w2_g11")
-        for c in range(3):
-            round_w4(0, w4_g0[:, c * KP : (c + 1) * KP], c, (nc.scalar.copy, nc.scalar.copy, gpsimd_round)[c])
+        w4_g0 = alloc("w4_g0", [P, PACK * N], BF16, "w2_g100")
+        round_w4(0, w4_g0[:, 0:KP], 0, nc.scalar.copy)
+        round_w4(0, w4_g0[:, KP : 2 * KP], 1, nc.scalar.copy)
+        late = alloc("w4_g0late", [P, KP], BF16, "w2_g113")
+        round_w4(0, late[:], 2, gpsimd_round)
         h_g10 = square(root1[:, 0], alloc("h_g10", [P, PACK * HALF], BF16, "w4_raw0")[:])
         h_g11 = square(root1[:, 1], alloc("h_g11", [P, PACK * HALF], BF16)[:])
-        quantise_w4(0, w4_g0, "damp5")
-        quantise_h(0, 0, h_g00, "damp4")
-        quantise_h(1, 0, h_g10, "h_g00")
-        w4_g1 = [alloc("w4_g1%d" % c, [P, PACK * P], BF16, "damp6", 2 * PACK * P * c) for c in range(3)]
+        w4_c[0] = alloc("w4_c0", [P, N], U32, "damp2")
+        w4_s[0] = alloc("w4_s0", [P, N], U8)
+        nc.vector.quantize_mx(w4_c[0][:, 0 : 2 * P].bitcast(FP8X4), w4_s[0][:, 0 : 2 * P], w4_g0[:, 0 : 2 * KP])
+        nc.vector.quantize_mx(w4_c[0][:, 2 * P : N].bitcast(FP8X4), w4_s[0][:, 2 * P : N], late[:])
+        quantise_h(1, 0, h_g10, "w4_g0")
+        w4_g1 = [alloc("w4_g1%d" % c, [P, PACK * P], BF16, "damp3", 2 * PACK * P * c) for c in range(3)]
         w4_c[1] = alloc("w4_c1", [P, N], U32)
         w4_s[1] = alloc("w4_s1", [P, N], U8)
 
@@ -372,7 +367,7 @@ def tile_list_solvent_docking_rescoring_kernel(
         quantise_w4_tile(2)
 
         for t in range(4):
-            pocket_pass(bank(4 + t, "warm%d" % t), 1, t, 1, True, True)
+            pocket_pass(bank(4 + t, "warm%d" % t)[:], 1, t, 1, every, True, True)
 
         accs = [[bank(3 * half + c, "y%d%d" % (half, c)) for c in range(3)] for half in range(2)]
 
@@ -396,6 +391,7 @@ def tile_list_solvent_docking_rescoring_kernel(
                 nc.scalar.activation(results[c][:, js], accs[half][c][:, 0:HALF], ACT.Identity, bias=bias_cols[:, c : c + 1])
             else:
                 nc.vector.tensor_scalar(results[c][:, js], accs[half][c][:, 0:HALF], bias_cols[:, c : c + 1], None, ALU.add)
-            if c < 2:
-                nc.sync.dma_start(out[c * P : (c + 1) * P, js], results[c][:, js])
-        nc.sync.dma_start(out[2 * P : 3 * P, :], results[2][:])
+            if c == 0:
+                nc.sync.dma_start(out[0:P, js], results[0][:, js])
+            elif half == 1:
+                nc.sync.dma_start(out[c * P : (c + 1) * P, :], results[c][:])

@@ -108,6 +108,11 @@ def tile_list_solvent_docking_rescoring_kernel(
         tab2_plane = zeroed_plane(nc.vector, "tab2_plane", T2)
         w1_plane = zeroed_plane(nc.vector, "w1_plane", 2 * H)
         v_moved = zeroed_plane(nc.vector, "v_moved", S)
+        minus_one = []
+        for a in range(2):
+            minus_one.append(alloc("minus_one%d" % a, [P, 1], F32))
+            places["end"] = places["end"] + 2 * PACK * HALF
+            nc.vector.memset(minus_one[a][:], -1.0)
         ident = alloc("ident", [P, P], F32)
         make_identity(nc, ident[:])
 
@@ -195,7 +200,7 @@ def tile_list_solvent_docking_rescoring_kernel(
 
         w2_g = {}
 
-        def round_w2(b, a, engines, pieces=1):
+        def round_w2(b, a, engines, pieces=1, sign=-1.0):
             width = PACK * KP // pieces
             grouped = [alloc("w2_g%d%d%d" % (b, a, i), [P, width], BF16) for i in range(pieces)]
             src = w2_raw[(b, a)][0][:].rearrange("p j (m t l) -> p t m j l", t=4, l=4)
@@ -210,8 +215,9 @@ def tile_list_solvent_docking_rescoring_kernel(
                         -1.0, 0.0, ALU.mult, ALU.add,
                     )
                 else:
-                    nc.scalar.activation(dst, src[:, t], ACT.Copy, scale=-1.0)
+                    nc.scalar.activation(dst, src[:, t], ACT.Copy, scale=sign if t == engines.index("s") else -1.0)
             w2_g[(b, a)] = grouped
+            places["end"] = places["end"] + 2048
             w2_c[(b, a)] = alloc("w2_c%d%d" % (b, a), [P, KP], U32)
             w2_s[(b, a)] = alloc("w2_s%d%d" % (b, a), [P, KP], U8)
 
@@ -320,35 +326,31 @@ def tile_list_solvent_docking_rescoring_kernel(
                     root0[:, half, 2 * pair : 2 * pair + 2, :], diff0[half][pair][:].rearrange("p (t j) -> p t j", t=2),
                     damp[pair][:, :, halves[half]], ALU.mult,
                 )
-        h_g00 = square(root0[:, 0], alloc("h_g00", [P, PACK * HALF], BF16)[:])
-        h_g01 = square(root0[:, 1], alloc("h_g01", [P, PACK * HALF], BF16)[:])
-        round_w2(1, 0, "vvgv", 2)
-        for piece in (1, 0):
+        round_w2(1, 0, "ssgv", 2, minus_one[0][:])
+        h_g00 = square(root0[:, 0], alloc("h_g00", [P, PACK * HALF], BF16, "minus_one0")[:])
+        for piece in range(2):
             quantise_w2(1, 0, piece)
-        for t in (2, 3, 0, 1):
+        for t in range(4):
             pocket_pass(diff1[t][:], 1, t, 0, every, False, False)
-        round_w2(1, 1, "vvss", 4)
+        round_w2(1, 1, "vvss", 4, minus_one[1][:])
+        h_g01 = square(root0[:, 1], alloc("h_g01", [P, PACK * HALF], BF16, "minus_one1")[:])
         quantise_w2(1, 1, 0)
         quantise_w2(1, 1, 1)
-        quantise_w2(1, 1, 2)
         quantise_h(0, 0, h_g00, "w2_g110")
+        quantise_w2(1, 1, 2)
         quantise_w2(1, 1, 3)
-        quantise_h(0, 1, h_g01, "w2_g112")
         for t in range(4):
             pocket_pass(diff1[t][:], 1, t, 1, every, False, True)
         make_root(1, 0, diff1, root1)
         make_root(1, 1, diff1, root1)
-        w4_g0 = alloc("w4_g0", [P, PACK * N], BF16, "w2_g100")
+        w4_g0 = alloc("w4_g0", [P, PACK * N], BF16, "w2_g113")
         round_w4(0, w4_g0[:, 0:KP], 0, nc.scalar.copy)
-        round_w4(0, w4_g0[:, KP : 2 * KP], 1, nc.scalar.copy)
-        late = alloc("w4_g0late", [P, KP], BF16, "w2_g113")
-        round_w4(0, late[:], 2, gpsimd_round)
-        h_g10 = square(root1[:, 0], alloc("h_g10", [P, PACK * HALF], BF16, "w4_raw0")[:])
+        round_w4(0, w4_g0[:, KP : 2 * KP], 1, gpsimd_round)
+        round_w4(0, w4_g0[:, 2 * KP : 3 * KP], 2, gpsimd_round)
+        h_g10 = square(root1[:, 0], alloc("h_g10", [P, PACK * HALF], BF16)[:])
         h_g11 = square(root1[:, 1], alloc("h_g11", [P, PACK * HALF], BF16)[:])
-        w4_c[0] = alloc("w4_c0", [P, N], U32, "damp2")
-        w4_s[0] = alloc("w4_s0", [P, N], U8)
-        nc.vector.quantize_mx(w4_c[0][:, 0 : 2 * P].bitcast(FP8X4), w4_s[0][:, 0 : 2 * P], w4_g0[:, 0 : 2 * KP])
-        nc.vector.quantize_mx(w4_c[0][:, 2 * P : N].bitcast(FP8X4), w4_s[0][:, 2 * P : N], late[:])
+        quantise_h(0, 1, h_g01, "damp2", 2048)
+        quantise_w4(0, w4_g0, "damp2")
         quantise_h(1, 0, h_g10, "w4_g0")
         w4_g1 = [alloc("w4_g1%d" % c, [P, PACK * P], BF16, "damp3", 2 * PACK * P * c) for c in range(3)]
         w4_c[1] = alloc("w4_c1", [P, N], U32)
@@ -359,9 +361,9 @@ def tile_list_solvent_docking_rescoring_kernel(
             nc.vector.quantize_mx(w4_c[1][:, ns].bitcast(FP8X4), w4_s[1][:, ns], w4_g1[c][:])
 
         round_w4(1, w4_g1[0][:], 0, nc.vector.tensor_copy)
+        quantise_w4_tile(0)
         round_w4(1, w4_g1[1][:], 1, nc.vector.tensor_copy)
         round_w4(1, w4_g1[2][:], 2, nc.scalar.copy)
-        quantise_w4_tile(0)
         quantise_h(1, 1, h_g11, "w4_g10")
         quantise_w4_tile(1)
         quantise_w4_tile(2)

@@ -108,11 +108,6 @@ def tile_list_solvent_docking_rescoring_kernel(
         tab2_plane = zeroed_plane(nc.vector, "tab2_plane", T2)
         w1_plane = zeroed_plane(nc.vector, "w1_plane", 2 * H)
         v_moved = zeroed_plane(nc.vector, "v_moved", S)
-        minus_one = []
-        for a in range(2):
-            minus_one.append(alloc("minus_one%d" % a, [P, 1], F32))
-            places["end"] = places["end"] + 2 * PACK * HALF
-            nc.vector.memset(minus_one[a][:], -1.0)
         ident = alloc("ident", [P, P], F32)
         make_identity(nc, ident[:])
 
@@ -200,9 +195,12 @@ def tile_list_solvent_docking_rescoring_kernel(
 
         w2_g = {}
 
-        def round_w2(b, a, engines, pieces=1, sign=-1.0):
+        def round_w2(b, a, engines, pieces=1):
             width = PACK * KP // pieces
-            grouped = [alloc("w2_g%d%d%d" % (b, a, i), [P, width], BF16) for i in range(pieces)]
+            grouped = []
+            for i in range(pieces):
+                grouped.append(alloc("w2_g%d%d%d" % (b, a, i), [P, width], BF16))
+                places["end"] = places["end"] + (2048 if pieces == 4 else 0)
             src = w2_raw[(b, a)][0][:].rearrange("p j (m t l) -> p t m j l", t=4, l=4)
             for t in range(4):
                 c0 = t * KP % width
@@ -215,9 +213,8 @@ def tile_list_solvent_docking_rescoring_kernel(
                         -1.0, 0.0, ALU.mult, ALU.add,
                     )
                 else:
-                    nc.scalar.activation(dst, src[:, t], ACT.Copy, scale=sign if t == engines.index("s") else -1.0)
+                    nc.scalar.activation(dst, src[:, t], ACT.Copy, scale=-1.0)
             w2_g[(b, a)] = grouped
-            places["end"] = places["end"] + 2048
             w2_c[(b, a)] = alloc("w2_c%d%d" % (b, a), [P, KP], U32)
             w2_s[(b, a)] = alloc("w2_s%d%d" % (b, a), [P, KP], U8)
 
@@ -326,30 +323,30 @@ def tile_list_solvent_docking_rescoring_kernel(
                     root0[:, half, 2 * pair : 2 * pair + 2, :], diff0[half][pair][:].rearrange("p (t j) -> p t j", t=2),
                     damp[pair][:, :, halves[half]], ALU.mult,
                 )
-        round_w2(1, 0, "ssgv", 2, minus_one[0][:])
-        h_g00 = square(root0[:, 0], alloc("h_g00", [P, PACK * HALF], BF16, "minus_one0")[:])
+        round_w2(1, 0, "sgvv", 2)
+        h_g00 = square(root0[:, 0], alloc("h_g00", [P, PACK * HALF], BF16, "damp0")[:])
+        h_g01 = square(root0[:, 1], alloc("h_g01", [P, PACK * HALF], BF16)[:])
         for piece in range(2):
             quantise_w2(1, 0, piece)
         for t in range(4):
             pocket_pass(diff1[t][:], 1, t, 0, every, False, False)
-        round_w2(1, 1, "vvss", 4, minus_one[1][:])
-        h_g01 = square(root0[:, 1], alloc("h_g01", [P, PACK * HALF], BF16, "minus_one1")[:])
+        round_w2(1, 1, "vvvs", 4)
         quantise_w2(1, 1, 0)
         quantise_w2(1, 1, 1)
-        quantise_h(0, 0, h_g00, "w2_g110")
         quantise_w2(1, 1, 2)
+        quantise_h(0, 0, h_g00, "w2_g110")
         quantise_w2(1, 1, 3)
+        quantise_h(0, 1, h_g01, "w2_g112")
         for t in range(4):
             pocket_pass(diff1[t][:], 1, t, 1, every, False, True)
         make_root(1, 0, diff1, root1)
         make_root(1, 1, diff1, root1)
-        w4_g0 = alloc("w4_g0", [P, PACK * N], BF16, "w2_g113")
-        round_w4(0, w4_g0[:, 0:KP], 0, nc.scalar.copy)
-        round_w4(0, w4_g0[:, KP : 2 * KP], 1, gpsimd_round)
-        round_w4(0, w4_g0[:, 2 * KP : 3 * KP], 2, gpsimd_round)
-        h_g10 = square(root1[:, 0], alloc("h_g10", [P, PACK * HALF], BF16)[:])
-        h_g11 = square(root1[:, 1], alloc("h_g11", [P, PACK * HALF], BF16)[:])
-        quantise_h(0, 1, h_g01, "damp2", 2048)
+        w4_g0 = alloc("w4_g0", [P, PACK * N], BF16)
+        nc.scalar.copy(
+            w4_g0[:].rearrange("p (n l t) -> p n t l", l=4, t=PACK), w4_raw[0][:].rearrange("p t (n l) -> p n t l", l=4)
+        )
+        h_g10 = square(root1[:, 0], alloc("h_g10", [P, PACK * HALF], BF16, "w4_raw0")[:])
+        h_g11 = square(root1[:, 1], alloc("h_g11", [P, PACK * HALF], BF16, "w4_raw0", 2048)[:])
         quantise_w4(0, w4_g0, "damp2")
         quantise_h(1, 0, h_g10, "w4_g0")
         w4_g1 = [alloc("w4_g1%d" % c, [P, PACK * P], BF16, "damp3", 2 * PACK * P * c) for c in range(3)]
@@ -361,9 +358,9 @@ def tile_list_solvent_docking_rescoring_kernel(
             nc.vector.quantize_mx(w4_c[1][:, ns].bitcast(FP8X4), w4_s[1][:, ns], w4_g1[c][:])
 
         round_w4(1, w4_g1[0][:], 0, nc.vector.tensor_copy)
-        quantise_w4_tile(0)
         round_w4(1, w4_g1[1][:], 1, nc.vector.tensor_copy)
         round_w4(1, w4_g1[2][:], 2, nc.scalar.copy)
+        quantise_w4_tile(0)
         quantise_h(1, 1, h_g11, "w4_g10")
         quantise_w4_tile(1)
         quantise_w4_tile(2)

@@ -336,18 +336,24 @@ def tile_list_solvent_docking_rescoring_kernel(
         quantise_w2(1, 1, 2)
         quantise_h(0, 0, h_g00, "w2_g110")
         quantise_w2(1, 1, 3)
-        quantise_h(0, 1, h_g01, "w2_g112")
         for t in range(4):
             pocket_pass(diff1[t][:], 1, t, 1, every, False, True)
         make_root(1, 0, diff1, root1)
         make_root(1, 1, diff1, root1)
-        w4_g0 = alloc("w4_g0", [P, PACK * N], BF16)
+        w4_g0 = alloc("w4_g0", [P, 2 * KP], BF16)
         nc.scalar.copy(
-            w4_g0[:].rearrange("p (n l t) -> p n t l", l=4, t=PACK), w4_raw[0][:].rearrange("p t (n l) -> p n t l", l=4)
+            w4_g0[:].rearrange("p (n l t) -> p n t l", l=4, t=PACK),
+            w4_raw[0][:, :, 0 : 2 * P].rearrange("p t (n l) -> p n t l", l=4),
         )
+        late = alloc("w4_g0late", [P, KP], BF16, "w2_g113")
+        round_w4(0, late[:], 2, gpsimd_round)
         h_g10 = square(root1[:, 0], alloc("h_g10", [P, PACK * HALF], BF16, "w4_raw0")[:])
         h_g11 = square(root1[:, 1], alloc("h_g11", [P, PACK * HALF], BF16, "w4_raw0", 2048)[:])
-        quantise_w4(0, w4_g0, "damp2")
+        quantise_h(0, 1, h_g01, "damp2", 2048)
+        w4_c[0] = alloc("w4_c0", [P, N], U32, "damp2")
+        w4_s[0] = alloc("w4_s0", [P, N], U8)
+        nc.vector.quantize_mx(w4_c[0][:, 0 : 2 * P].bitcast(FP8X4), w4_s[0][:, 0 : 2 * P], w4_g0[:])
+        nc.vector.quantize_mx(w4_c[0][:, 2 * P : N].bitcast(FP8X4), w4_s[0][:, 2 * P : N], late[:])
         quantise_h(1, 0, h_g10, "w4_g0")
         w4_g1 = [alloc("w4_g1%d" % c, [P, PACK * P], BF16, "damp3", 2 * PACK * P * c) for c in range(3)]
         w4_c[1] = alloc("w4_c1", [P, N], U32)
@@ -390,7 +396,7 @@ def tile_list_solvent_docking_rescoring_kernel(
                 nc.scalar.activation(results[c][:, js], accs[half][c][:, 0:HALF], ACT.Identity, bias=bias_cols[:, c : c + 1])
             else:
                 nc.vector.tensor_scalar(results[c][:, js], accs[half][c][:, 0:HALF], bias_cols[:, c : c + 1], None, ALU.add)
-            if c == 0:
-                nc.sync.dma_start(out[0:P, js], results[0][:, js])
+            if c < 2:
+                nc.sync.dma_start(out[c * P : (c + 1) * P, js], results[c][:, js])
             elif half == 1:
                 nc.sync.dma_start(out[c * P : (c + 1) * P, :], results[c][:])

@@ -229,9 +229,9 @@ def tile_list_solvent_docking_rescoring_kernel(
         nc.gpsimd.dma_start(v_moved[0:LIVE_ROWS, :].bitcast(I32), v_packed[4 : 4 + LIVE_ROWS, :].bitcast(I32))
         v_s = [v_packed, v_moved]
         v2_w = [gather("v2_w%d" % a, tab2_w[:, a * T2 : (a + 1) * T2], idx2, U32) for a in range(2)]
-        v2_s = gather("v2_s", tab2_plane[:], idx2, U8, "tab2_w")
         w1_o = reorder("w1_o", w1_w, 2 * 2 * H, U8, 2)
         w1_s = reorder_plane("w1_s", w1_plane, 2 * H)
+        v2_s = gather("v2_s", tab2_plane[:], idx2, U8, "w1_plane")
         round_w2(0, 0, "vsss")
         quantise_w2(0, 0)
         round_w2(0, 1, "vvss", 2)

@@ -232,8 +232,9 @@ def tile_list_solvent_docking_rescoring_kernel(
         w1_o = reorder("w1_o", w1_w, 2 * 2 * H, U8, 2)
         w1_s = reorder_plane("w1_s", w1_plane, 2 * H)
         v2_s = gather("v2_s", tab2_plane[:], idx2, U8, "w1_plane")
-        round_w2(0, 0, "vsss")
-        quantise_w2(0, 0)
+        round_w2(0, 0, "vsss", 2)
+        quantise_w2(0, 0, 0)
+        quantise_w2(0, 0, 1)
         round_w2(0, 1, "vvss", 2)
         quantise_w2(0, 1, 0)
         quantise_w2(0, 1, 1)
@@ -309,12 +310,15 @@ def tile_list_solvent_docking_rescoring_kernel(
                     one_pass(acc, 0, t, a, halves[half], start and t % 2 == 0, stop and t % 2 == 1)
 
         first_group(ligand_pass, 0, True, False)
+        for t in range(2):
+            ligand_pass(diff1[t][:], 1, t, 0, every, True, False)
         first_group(pocket_pass, 0, False, False)
         first_group(pocket_pass, 1, False, False)
         first_group(ligand_pass, 1, False, True)
-        for a in (1, 0):
-            for t in range(4):
-                ligand_pass(diff1[t][:], 1, t, a, every, a == 1, False)
+        for t in range(4):
+            ligand_pass(diff1[t][:], 1, t, 1, every, t >= 2, False)
+        for t in range(2, 4):
+            ligand_pass(diff1[t][:], 1, t, 0, every, False, False)
         root0 = alloc("root0", [P, 2, PACK, HALF], F32)
         root1 = alloc("root1", [P, 2, PACK, HALF], F32)
         for half in range(2):

@@ -375,9 +375,6 @@ def tile_list_solvent_docking_rescoring_kernel(
         quantise_w4_tile(1)
         quantise_w4_tile(2)
 
-        for t in range(4):
-            pocket_pass(bank(4 + t, "warm%d" % t)[:], 1, t, 1, every, True, True)
-
         accs = [[bank(3 * half + c, "y%d%d" % (half, c)) for c in range(3)] for half in range(2)]
 
         def output_pass(b, half, c):

@@ -232,7 +232,7 @@ def tile_list_solvent_docking_rescoring_kernel(
         w1_o = reorder("w1_o", w1_w, 2 * 2 * H, U8, 2)
         w1_s = reorder_plane("w1_s", w1_plane, 2 * H)
         v2_s = gather("v2_s", tab2_plane[:], idx2, U8, "w1_plane")
-        round_w2(0, 0, "vsss", 2)
+        round_w2(0, 0, "vvss", 2)
         quantise_w2(0, 0, 0)
         quantise_w2(0, 0, 1)
         round_w2(0, 1, "vvss", 2)

from contextlib import ExitStack

import concourse.mybir as mybir
from concourse.masks import make_identity

K, K3, H, N, T, T2, T3, S = 1024, 512, 1024, 384, 2048, 1024, 2048, 512
FLOPS = 2 * S * (2 * K * H + K3 * H + H * N)

F32 = mybir.dt.float32
BF16 = mybir.dt.bfloat16
I32 = mybir.dt.int32
U32 = mybir.dt.uint32
U16 = mybir.dt.uint16
U8 = mybir.dt.uint8
BYTES_OF = {F32: 4, BF16: 2, U32: 4, U16: 2, U8: 1}
FP8X4 = mybir.dt.float8_e4m3fn_x4
FP4X4 = mybir.dt.float4_e2m1fn_x4
ACT = mybir.ActivationFunctionType
ALU = mybir.AluOpType

P = 128
PACK = 4
KP = P * PACK
HALF = S // 2
TAB2_ROW = 8
TAB_ROW = 0
LIVE_ROWS = 100


def tile_list_solvent_docking_rescoring_kernel(
    tc, tab_words, tab_scales, tab2_words, tab2_scales, tab3_words, tab3_scales, offs, offs2, offs3,
    w1_words, w1_scales, w2, w3_words, w3_scales, gain, w4, bias, out,
):
    nc = tc.nc
    with ExitStack() as ctx:
        lists = ctx.enter_context(tc.tile_pool(name="lists", bufs=1))
        sb = ctx.enter_context(tc.tile_pool(name="sb", bufs=1))
        psum = ctx.enter_context(tc.psum_pool(name="psum", bufs=1))

        places = {"end": 0}

        def alloc(name, shape, dtype, slot=None, at=0):
            if slot is None:
                places[name] = places["end"]
                size = BYTES_OF[dtype]
                for extent in shape[1:]:
                    size = size * extent
                places["end"] = places[name] + (size + 63) // 64 * 64
            else:
                places[name] = places[slot] + at
            return sb.tile(shape, dtype, name=name, align_bytes=64, offset=places[name])

        def bank(index, name):
            return psum.tile([P, S], F32, name=name, tag="bank%d" % index)

        def zeroed_plane(engine, name, width):
            plane = alloc(name, [P, width], U8)
            engine.memset(plane[:].bitcast(I32), 0)
            return plane

        def load_list(name, src):
            offsets = lists.tile([P, S // 16], U16, name=name)
            nc.sync.dma_start(offsets[:], src)
            return offsets

        def load_scale_rows(queue, plane, scales):
            passes = scales.shape[0]
            rows = scales.bitcast(I32).rearrange("a (q r) w -> r q a w", r=4)
            for r in range(4):
                queue.dma_start(plane[r:P:32, :].bitcast(I32).rearrange("q (a w) -> q a w", a=passes), rows[r])

        def load_packed_rows(queue, plane, scales, row):
            rows = scales.bitcast(I32)
            for q in range(4):
                queue.dma_start(plane[32 * q + row : 32 * q + row + 8, :].bitcast(I32), rows[:, 4 * q : 4 * q + 4, :])

        def load_words(name, src, width, dtype):
            words = alloc(name, [P, width], dtype)
            nc.sync.dma_start(words[:].bitcast(I32), src.bitcast(I32))
            return words

        def gather(name, window, offsets, dtype, slot=None):
            picked = alloc(name, [P, S], dtype, slot)
            nc.vector.tensor_copy(picked[:], window.indirect(offsets[:]))
            return picked

        def reorder(name, src, width, dtype, run):
            ordered = alloc(name, [P, width], dtype)
            nc.vector.tensor_copy(
                ordered[:].bitcast(I32).rearrange("p (g t m w) -> p g t m w", t=4, m=32, w=run),
                src[:].bitcast(I32).rearrange("p (g m t w) -> p g t m w", t=4, m=32, w=run),
            )
            return ordered

        def reorder_plane(name, src, width, slot=None):
            ordered = alloc(name, [P, width], U8, slot)
            nc.vector.tensor_copy(
                ordered[:].bitcast(I32).rearrange("p (g t x m) -> p g x t m", t=4, x=8, m=4),
                src[:].bitcast(I32).rearrange("p (g x m t) -> p g x t m", t=4, x=8, m=4),
            )
            return ordered

        tab_plane = zeroed_plane(nc.vector, "tab_plane", T)
        tab3_plane = zeroed_plane(nc.vector, "tab3_plane", T3)
        rows = alloc("rows", [P, 4 * P], F32)
        nc.vector.memset(rows[:], 0.0)
        w3_plane = zeroed_plane(nc.vector, "w3_plane", H)
        tab2_plane = zeroed_plane(nc.vector, "tab2_plane", T2)
        w1_plane = zeroed_plane(nc.vector, "w1_plane", 2 * H)
        v_moved = zeroed_plane(nc.vector, "v_moved", S)
        ident = alloc("ident", [P, P], F32)
        make_identity(nc, ident[:])

        tab_w = [None, None]
        w2_raw = {}
        w4_raw = [None, None]

        def load_w2(b, a, parts=1):
            width = KP // parts
            w2_raw[(b, a)] = []
            for part in range(parts):
                raw = alloc("w2_raw%d%d%d" % (b, a, part), [P, PACK, width], F32)
                c0 = b * KP + part * width
                nc.sync.dma_start(raw[:], w2[a * KP : (a + 1) * KP, c0 : c0 + width].rearrange("(p j) c -> p j c", j=PACK))
                w2_raw[(b, a)].append(raw)

        def load_w4(b):
            raw = alloc("w4_raw%d" % b, [P, PACK, N], F32)
            src = w4[b * KP : (b + 1) * KP, :].rearrange("(m t l) n -> t m l n", t=4, l=4)
            for t in range(4):
                nc.sync.dma_start(raw[:, t, :], src[t])
            w4_raw[b] = raw

        load_packed_rows(nc.gpsimd, tab_plane, tab_scales, TAB_ROW)
        load_packed_rows(nc.gpsimd, tab2_plane, tab2_scales, TAB2_ROW)
        tab3_w = load_words("tab3_w", tab3_words[0], T3, U16)
        gain_rows = alloc("gain_rows", [2, KP], F32)
        nc.sync.dma_start(gain_rows[:], gain.rearrange("(b c) -> b c", b=2))
        w3_w = load_words("w3_w", w3_words[0].rearrange("p c i -> p (c i)"), H, U32)
        idx3 = load_list("idx3", offs3)
        load_scale_rows(nc.sync, tab3_plane, tab3_scales)
        nc.sync.dma_start(rows[2:3, 0:N], bias.rearrange("(c n) -> c n", c=1))
        tab_w[0] = load_words("tab_w0", tab_words[0].rearrange("p c i -> p (c i)"), T, U32)
        load_scale_rows(nc.sync, w3_plane, w3_scales)
        idx = load_list("idx", offs)
        tab2_w = alloc("tab2_w", [P, 2 * T2], U32)
        nc.sync.dma_start(
            tab2_w[:].bitcast(I32).rearrange("p (a w) -> p a w", a=2),
            tab2_words.rearrange("a p c i -> p a (c i)").bitcast(I32),
        )
        idx2 = load_list("idx2", offs2)
        w1_w = alloc("w1_w", [P, 2 * 2 * H], U8)
        nc.sync.dma_start(
            w1_w[:].bitcast(I32).rearrange("p (a w) -> p a w", a=2), w1_words.bitcast(I32).rearrange("a p w -> p a w")
        )
        load_scale_rows(nc.sync, w1_plane, w1_scales)
        load_w2(0, 0)
        load_w2(0, 1)
        tab_w[1] = load_words("tab_w1", tab_words[1].rearrange("p c i -> p (c i)"), T, U32)
        load_w2(1, 0)
        load_w2(1, 1)
        load_w4(0)
        load_w4(1)

        nc.scalar.activation(
            rows[0:2, :].rearrange("b (t m l) -> b t m l", t=4, l=4),
            gain_rows[:].rearrange("b (m t l) -> b t m l", t=4, l=4), ACT.Ln,
        )
        turned = bank(7, "turned")
        for t in range(4):
            nc.tensor.transpose(turned[:, t * P : (t + 1) * P], rows[:, t * P : (t + 1) * P], ident[:])
        columns = turned[:].rearrange("p (t c) -> p t c", t=4)
        half_log = alloc("half_log", [P, 4, 2], F32)
        nc.scalar.activation(half_log[:], columns[:, :, 0:2], ACT.Copy, scale=0.5)
        bias_cols = alloc("bias_cols", [P, 3], F32)
        nc.scalar.copy(bias_cols[:], columns[:, 0:3, 2])

        v3_w = gather("v3_w", tab3_w[:], idx3, U16)
        w3_o = reorder("w3_o", w3_w, H, U32, 4)
        v3_s = gather("v3_s", tab3_plane[:], idx3, U8)
        w3_s = reorder_plane("w3_s", w3_plane, H)
        damp = [alloc("damp%d" % pair, [P, 2, S], F32) for pair in range(4)]
        for g in range(8):
            cs = slice(g * P, (g + 1) * P)
            sol = bank(g, "sol%d" % g)
            nc.tensor.matmul_mx(
                sol[:], lhsT=w3_o[:, cs].bitcast(FP8X4), lhsT_scale=w3_s[:, cs],
                rhs=v3_w[:].bitcast(FP4X4), rhs_scale=v3_s[:], start=True, stop=True,
            )
            nc.scalar.activation(damp[g // 2][:, g % 2, :], sol[:], ACT.Exp, bias=half_log[:, g % 4, g // 4 : g // 4 + 1], scale=0.5)


        w2_c = {}
        w2_s = {}

        w2_g = {}

        def round_w2(b, a, engines, pieces=1):
            width = PACK * KP // pieces
            grouped = []
            for i in range(pieces):
                grouped.append(alloc("w2_g%d%d%d" % (b, a, i), [P, width], BF16))
                places["end"] = places["end"] + (2048 if pieces == 4 else 0)
            src = w2_raw[(b, a)][0][:].rearrange("p j (m t l) -> p t m j l", t=4, l=4)
            for t in range(4):
                c0 = t * KP % width
                dst = grouped[t * KP // width][:, c0 : c0 + KP].rearrange("p (m l j) -> p m j l", l=4, j=PACK)
                if engines[t] == "v":
                    nc.vector.tensor_scalar(dst, src[:, t], -1.0, None, ALU.mult)
                elif engines[t] == "g":
                    nc.gpsimd.tensor_scalar(
                        dst.rearrange("p m j l -> p m l j"), src[:, t].rearrange("p m j l -> p m l j"),
                        -1.0, 0.0, ALU.mult, ALU.add,
                    )
                else:
                    nc.scalar.activation(dst, src[:, t], ACT.Copy, scale=-1.0)
            w2_g[(b, a)] = grouped
            w2_c[(b, a)] = alloc("w2_c%d%d" % (b, a), [P, KP], U32)
            w2_s[(b, a)] = alloc("w2_s%d%d" % (b, a), [P, KP], U8)

        def quantise_w2(b, a, piece=0):
            width = KP // len(w2_g[(b, a)])
            cs = slice(piece * width, (piece + 1) * width)
            nc.vector.quantize_mx(w2_c[(b, a)][:, cs].bitcast(FP8X4), w2_s[(b, a)][:, cs], w2_g[(b, a)][piece][:])

        v_w = [None, None]
        v_w[0] = gather("v_w0", tab_w[0][:], idx, U32)
        v_packed = gather("v_packed", tab_plane[:], idx, U8, "tab_w0")
        nc.gpsimd.dma_start(v_moved[0:LIVE_ROWS, :].bitcast(I32), v_packed[4 : 4 + LIVE_ROWS, :].bitcast(I32))
        v_s = [v_packed, v_moved]
        v2_w = [gather("v2_w%d" % a, tab2_w[:, a * T2 : (a + 1) * T2], idx2, U32) for a in range(2)]
        w1_o = reorder("w1_o", w1_w, 2 * 2 * H, U8, 2)
        w1_s = reorder_plane("w1_s", w1_plane, 2 * H)
        v2_s = gather("v2_s", tab2_plane[:], idx2, U8, "w1_plane")
        round_w2(0, 0, "vvss", 2)
        quantise_w2(0, 0, 0)
        quantise_w2(0, 0, 1)
        round_w2(0, 1, "vvss", 2)
        quantise_w2(0, 1, 0)
        quantise_w2(0, 1, 1)
        v_w[1] = alloc("v_w1", [P, S], U32)
        halves = [slice(half * HALF, (half + 1) * HALF) for half in range(2)]
        for half in range(2):
            nc.vector.tensor_copy(v_w[1][:, halves[half]], tab_w[1][:].indirect(idx[:, 16 * half : 16 * (half + 1)]))

        def ligand_pass(acc, b, t, a, js, start, stop):
            c0 = a * H + b * KP + t * P
            nc.tensor.matmul_mx(
                acc, lhsT=w1_o[:, 2 * c0 : 2 * (c0 + P)].bitcast(FP4X4), lhsT_scale=w1_s[:, c0 : c0 + P],
                rhs=v_w[a][:, js].bitcast(FP8X4), rhs_scale=v_s[a][:, js], start=start, stop=stop,
            )

        def pocket_pass(acc, b, t, a, js, start, stop):
            cs = slice(t * P, (t + 1) * P)
            nc.tensor.matmul_mx(
                acc, lhsT=w2_c[(b, a)][:, cs].bitcast(FP8X4), lhsT_scale=w2_s[(b, a)][:, cs],
                rhs=v2_w[a][:, js].bitcast(FP8X4), rhs_scale=v2_s[TAB2_ROW + 4 * a : P, js], start=start, stop=stop,
            )

        w4_c = [None, None]
        w4_s = [None, None]

        def round_w4(b, dst, c, copy):
            src = w4_raw[b][:, :, c * P : (c + 1) * P]
            copy(dst.rearrange("p (n l t) -> p n t l", l=4, t=PACK), src.rearrange("p t (n l) -> p n t l", l=4))

        def gpsimd_round(dst, src):
            nc.gpsimd.tensor_scalar(
                dst.rearrange("p n t l -> p n l t"), src.rearrange("p n t l -> p n l t"), 1.0, 0.0, ALU.mult, ALU.add
            )

        def quantise_w4(b, grouped, slot):
            codes = alloc("w4_c%d" % b, [P, N], U32, slot)
            scales = alloc("w4_s%d" % b, [P, N], U8)
            nc.vector.quantize_mx(codes[:].bitcast(FP8X4), scales[:], grouped[:])
            w4_c[b] = codes
            w4_s[b] = scales

        h_c = {}
        h_s = {}

        def make_root(b, half, diff, root):
            js = slice(half * HALF, (half + 1) * HALF)
            for t in range(4):
                nc.vector.tensor_tensor(root[:, half, t, :], diff[t][:, js], damp[2 * b + t // 2][:, t % 2, js], ALU.mult)

        def square(root, grouped):
            nc.scalar.activation(
                grouped.rearrange("p (c l t) -> p c t l", l=4, t=PACK),
                root.rearrange("p t (c l) -> p c t l", l=4),
                ACT.Square,
            )
            return grouped

        def quantise_h(b, half, grouped, slot, at=0):
            codes = alloc("h_c%d%d" % (b, half), [P, HALF], U32, slot, at)
            scales = alloc("h_s%d%d" % (b, half), [P, HALF], U8)
            nc.vector.quantize_mx(codes[:].bitcast(FP8X4), scales[:], grouped)
            h_c[(b, half)] = codes
            h_s[(b, half)] = scales

        every = slice(0, S)
        diff0 = [[bank(2 * half + pair, "diff0%d%d" % (half, pair)) for pair in range(2)] for half in range(2)]
        diff1 = [bank(4 + t, "diff1%d" % t) for t in range(4)]

        def first_group(one_pass, a, start, stop):
            for half in range(2):
                for t in range(4):
                    acc = diff0[half][t // 2][:, halves[t % 2]]
                    one_pass(acc, 0, t, a, halves[half], start and t % 2 == 0, stop and t % 2 == 1)

        first_group(ligand_pass, 0, True, False)
        for t in range(2):
            ligand_pass(diff1[t][:], 1, t, 0, every, True, False)
        first_group(pocket_pass, 0, False, False)
        first_group(pocket_pass, 1, False, False)
        first_group(ligand_pass, 1, False, True)
        for t in range(4):
            ligand_pass(diff1[t][:], 1, t, 1, every, t >= 2, False)
        for t in range(2, 4):
            ligand_pass(diff1[t][:], 1, t, 0, every, False, False)
        root0 = alloc("root0", [P, 2, PACK, HALF], F32)
        root1 = alloc("root1", [P, 2, PACK, HALF], F32)
        for half in range(2):
            for pair in range(2):
                nc.vector.tensor_tensor(
                    root0[:, half, 2 * pair : 2 * pair + 2, :], diff0[half][pair][:].rearrange("p (t j) -> p t j", t=2),
                    damp[pair][:, :, halves[half]], ALU.mult,
                )
        round_w2(1, 0, "sgvv", 2)
        h_g00 = square(root0[:, 0], alloc("h_g00", [P, PACK * HALF], BF16, "damp0")[:])
        h_g01 = square(root0[:, 1], alloc("h_g01", [P, PACK * HALF], BF16)[:])
        for piece in range(2):
            quantise_w2(1, 0, piece)
        for t in range(4):
            pocket_pass(diff1[t][:], 1, t, 0, every, False, False)
        round_w2(1, 1, "vvvs", 4)
        quantise_w2(1, 1, 0)
        quantise_w2(1, 1, 1)
        quantise_w2(1, 1, 2)
        quantise_h(0, 0, h_g00, "w2_g110")
        quantise_w2(1, 1, 3)
        for t in range(4):
            pocket_pass(diff1[t][:], 1, t, 1, every, False, True)
        make_root(1, 0, diff1, root1)
        make_root(1, 1, diff1, root1)
        w4_g0 = alloc("w4_g0", [P, 2 * KP], BF16)
        nc.scalar.copy(
            w4_g0[:].rearrange("p (n l t) -> p n t l", l=4, t=PACK),
            w4_raw[0][:, :, 0 : 2 * P].rearrange("p t (n l) -> p n t l", l=4),
        )
        late = alloc("w4_g0late", [P, KP], BF16, "w2_g113")
        round_w4(0, late[:], 2, gpsimd_round)
        h_g10 = square(root1[:, 0], alloc("h_g10", [P, PACK * HALF], BF16, "w4_raw0")[:])
        h_g11 = square(root1[:, 1], alloc("h_g11", [P, PACK * HALF], BF16, "w4_raw0", 2048)[:])
        quantise_h(0, 1, h_g01, "damp2", 2048)
        w4_c[0] = alloc("w4_c0", [P, N], U32, "damp2")
        w4_s[0] = alloc("w4_s0", [P, N], U8)
        nc.vector.quantize_mx(w4_c[0][:, 0 : 2 * P].bitcast(FP8X4), w4_s[0][:, 0 : 2 * P], w4_g0[:])
        nc.vector.quantize_mx(w4_c[0][:, 2 * P : N].bitcast(FP8X4), w4_s[0][:, 2 * P : N], late[:])
        quantise_h(1, 0, h_g10, "w4_g0")
        w4_g1 = [alloc("w4_g1%d" % c, [P, PACK * P], BF16, "damp3", 2 * PACK * P * c) for c in range(3)]
        w4_c[1] = alloc("w4_c1", [P, N], U32)
        w4_s[1] = alloc("w4_s1", [P, N], U8)

        def quantise_w4_tile(c):
            ns = slice(c * P, (c + 1) * P)
            nc.vector.quantize_mx(w4_c[1][:, ns].bitcast(FP8X4), w4_s[1][:, ns], w4_g1[c][:])

        round_w4(1, w4_g1[0][:], 0, nc.vector.tensor_copy)
        round_w4(1, w4_g1[1][:], 1, nc.vector.tensor_copy)
        round_w4(1, w4_g1[2][:], 2, nc.scalar.copy)
        quantise_w4_tile(0)
        quantise_h(1, 1, h_g11, "w4_g10")
        quantise_w4_tile(1)
        quantise_w4_tile(2)

        accs = [[bank(3 * half + c, "y%d%d" % (half, c)) for c in range(3)] for half in range(2)]

        def output_pass(b, half, c):
            ns = slice(c * P, (c + 1) * P)
            nc.tensor.matmul_mx(
                accs[half][c][:, 0:HALF],
                lhsT=w4_c[b][:, ns].bitcast(FP8X4), lhsT_scale=w4_s[b][:, ns],
                rhs=h_c[(b, half)][:].bitcast(FP8X4), rhs_scale=h_s[(b, half)][:],
                start=(b == 0), stop=(b == 1),
            )

        for half in range(2):
            for c in range(3):
                output_pass(0, half, c)
        results = [alloc("result%d" % c, [P, S], F32) for c in range(3)]
        for half, c in ((0, 0), (0, 1), (1, 0), (1, 1), (0, 2), (1, 2)):
            output_pass(1, half, c)
            js = slice(half * HALF, (half + 1) * HALF)
            if half == 0:
                nc.scalar.activation(results[c][:, js], accs[half][c][:, 0:HALF], ACT.Identity, bias=bias_cols[:, c : c + 1])
            else:
                nc.vector.tensor_scalar(results[c][:, js], accs[half][c][:, 0:HALF], bias_cols[:, c : c + 1], None, ALU.add)
            if c < 2:
                nc.sync.dma_start(out[c * P : (c + 1) * P, js], results[c][:, js])
            elif half == 1:
                nc.sync.dma_start(out[c * P : (c + 1) * P, :], results[c][:])
